import numpy as np, ml_dtypes
CORES = [35,38,43,46]
N = 4
BF = ml_dtypes.bfloat16
def gentries(a):
    return np.ascontiguousarray(a.reshape(8, 16, -1).transpose(0, 2, 1)).reshape(8, -1)
def gtable(e):
    e = np.asarray(e); return np.ascontiguousarray(e.reshape(8, -1, 16).transpose(0, 2, 1)).reshape(128, -1).astype(np.int32)
V, R = 4096, 6
def family(rng, sizes, depth, pool, mix, fall=None):
    key = np.tile(np.arange(V), (N, 1)); lev = np.zeros(V, np.int64); comp = np.zeros(V, np.int64); via = [-1] * V; o = rng.permutation(V); a = 0
    for i in range(len(sizes)):
        s, D = int(sizes[i]), int(depth[i]); m = o[a:a + s]; a += s; comp[m] = i
        if s == 1: continue
        root = int(np.min(m)); m = m[m != root]; l = np.concatenate([np.arange(1, D + 1), rng.integers(1, D + 1, s - 1 - D)])
        if fall is not None and fall[i]: m = np.sort(m)[::-1]; l = np.sort(l)
        lev[m] = l
        at = [[root]] + [[] for k in range(D)]
        for c, k in zip(m.tolist(), l.tolist()): at[k].append(c)
        for k in range(1, D + 1):
            for c in at[k]:
                p = at[k - 1][int(rng.integers(len(at[k - 1])))]; w = [q for q in pool if q != via[p]]; q = w[int(rng.integers(len(w)))]
                key[q, c] = key[q, p]; via[c] = q
    for q in range(N if mix > 0 else 0):
        h = np.flatnonzero(key[q] == np.arange(V)); t = comp[h] * (R + 1) + lev[h]; keep = rng.random(h.size) >= mix
        hk, tk = h[keep], t[keep]; s = np.argsort(tk, kind="stable"); hk, tk = hk[s], tk[s]
        lo = np.searchsorted(tk, t, "left"); n = np.searchsorted(tk, t, "right") - lo; z = ~keep & (n > 0)
        to = h + 0; to[z] = hk[lo[z] + (rng.random(np.count_nonzero(z)) * n[z]).astype(np.int64)]
        jump = np.arange(V); jump[h] = to; key[q] = jump[key[q]]
    return key
def lay(rng, key, way):
    if way == 0: o = np.lexsort((rng.random(V), rng.permutation(V)[key]))
    elif way == 1: o = np.lexsort((np.arange(V), key))
    else: o = np.lexsort((-np.arange(V), -key))
    k = key[o]; s = np.ones(V, np.int64); s[1:] = k[1:] != k[:-1]
    e = np.append(np.flatnonzero(s)[1:], V) - 1; last = np.zeros(V, np.int64); last[o] = e[np.add.accumulate(s) - 1]
    return [o, s, last]
def pack(rng, keys, ways):
    a = np.array([[lay(rng, keys[g][q], ways[q, g]) for g in range(8)] for q in range(N)])
    return {"pm": np.stack([gtable(u) for u in a[:, :, 0]]), "en": np.stack([gtable(u) for u in a[:, :, 2]]), "st": np.ascontiguousarray(a[:, :, 1]).astype(np.int32)}
def depths(rng, s):
    top = np.minimum(R, s - 1); D = np.where(top > 0, 1 + (rng.random(s.size) * top).astype(np.int64), 0); i = np.argmax(s); D[i] = top[i]; return D
def some(rng):
    out = []
    for n in rng.choice(np.arange(6, 41), 8, replace=False):
        c = np.sort(rng.choice(V - 1, int(n) - 1, replace=False)) + 1; s = np.diff(np.concatenate([[0], c, [V]]))
        out.append(family(rng, s, depths(rng, s), list(range(N)), rng.choice([0.0, 0.05, 0.15])))
    return out
def setup_inputs(rng):
    return pack(rng, some(rng), np.zeros((N, 8), np.int64))
def setup_inputs_deep(rng):
    few = rng.permutation(8)[:4]; n = rng.choice(np.arange(V // (2 * (R + 1)), V // (R + 1) + 1), 8, replace=False); keys = []
    for g in range(8):
        m = int(n[g]); s = [R + 1] * m + [1] * (V - m * (R + 1)); pool = rng.permutation(N)[:2].tolist() if g in few else list(range(N))
        keys.append(family(rng, s, [R] * m + [0] * (V - m * (R + 1)), pool, 0.0, np.arange(len(s)) % 2 == 0))
    return pack(rng, keys, np.zeros((N, 8), np.int64))
def setup_inputs_ends(rng):
    keys = some(rng); w = rng.permutation(8); one = np.tile(np.arange(V), (N, 1))
    keys[w[0]][rng.integers(N)] = 0
    keys[w[1]] = one + 0
    keys[w[2]] = np.tile(rng.integers(0, 30, V), (N, 1))
    keys[w[3]] = one + 0; keys[w[3]][rng.integers(N)] = rng.integers(0, 3, V)
    x = np.concatenate([[0], 1 + rng.choice(V - 2, R - 1, replace=False), [V - 1]]); k = one + 0; ab = rng.permutation(N)[:2]
    for i in range(R): k[ab[i % 2], x[i + 1]] = x[i]
    keys[w[4]] = k
    return pack(rng, keys, np.zeros((N, 8), np.int64))
def setup_inputs_order(rng):
    return pack(rng, some(rng), rng.integers(1, 3, (N, 8)))
def setup_inputs_spread(rng):
    keys = []; half = int(rng.integers(8))
    for g in range(8):
        s = [1] * (V // 2 if g == half else 0); left = V - len(s)
        while left > 0:
            t = max(1, int(left * (0.3 + 0.4 * rng.random()))); s.append(t); left -= t
        s = np.array(s); keys.append(family(rng, s, depths(rng, s), list(range(N)) + [int(rng.integers(N))] * (3 * N), rng.choice([0.0, 0.3, 0.8])))
    return pack(rng, keys, np.zeros((N, 8), np.int64))
def hop(p, st, L):
    g = np.arange(8)[:, None]; M = L
    for q in range(N):
        s = st[q].reshape(-1); m = np.minimum.reduceat(L[g, p[q]].reshape(-1), np.flatnonzero(s))
        u = np.empty_like(L); u[g, p[q]] = m[np.add.accumulate(s) - 1].reshape(8, V); M = np.minimum(M, u)
    return M
def check_inputs(d):
    p = np.stack([gentries(a) for a in d["pm"]]); e = np.stack([gentries(a) for a in d["en"]]); s = d["st"]
    if not (np.sort(p, -1) == np.arange(V)).all(): return ["pm: every vertex once"]
    if not (((s == 0) | (s == 1)).all() and (s[:, :, 0] == 1).all()): return ["st: 0 and 1, beginning with 1"]
    bad = []; t = s.reshape(-1); last = ((np.append(np.flatnonzero(t)[1:], t.size) - 1) % V)[np.add.accumulate(t) - 1].reshape(N, 8, V)
    if not (np.take_along_axis(e, p, 2) == last).all(): bad.append("en: last places")
    L = np.tile(np.arange(V), (8, 1))
    for i in range(R): L = hop(p, s, L)
    if not (hop(p, s, L) == L).all(): bad.append("at most R steps to the smallest vertex")
    return bad
def reference(pm, en, st):
    p = np.stack([gentries(a) for a in pm]); L = np.tile(np.arange(V), (8, 1))
    while True:
        M = hop(p, st, L)
        if (M == L).all(): break
        L = M
    c = np.count_nonzero(L == np.arange(V), axis=1).reshape(8, 1)
    return {"y": np.stack([L[np.arange(8)[:, None], p[r]] for r in range(N)]).astype(np.float32), "cnt": np.stack([c for r in range(N)]).astype(np.float32)}

@@ -1,0 +1,403 @@
+from concourse.bass import DstId, RemoteDMATransfer
+from concourse.mybir import AluOpType, AxisListType, ActivationFunctionType
+import math
+
+V, R = 4096, 6
+PARTS = {"A": (0, 8, 15), "B": (15, 18, 18), "C": (18, 18, 23), "D": (23, 25, 28), "E": (28, 29, 32)}
+FIRST = {"V0": (0, 5), "V1": (5, 8), "S0": (8, 11), "S1": (11, 15)}
+WSHARE = {"B": 3, "C": 5, "D": 0, "E": 2}
+TURN = {"B": "psT1", "C": "psT2", "D": "psT1", "E": "psT2"}
+ORDER = "AgS0 AgV0 AgS1 CgS AgV1 BgV Bt DgV Ct Af Bf Ar DgS Cf Be Dt EgS Ce AwV EgV Df Et Ef De DwV CwS BwS Ee EwS EwV"
+CUTS = [0, 1344, 3328, 4096]
+BACK1 = (0, 7, 13, 16)
+LAST = (("psT0", 0, 8, 17), ("psT1", 17, 22, 28), ("psT2", 28, 30, 32))
+OFF = 12
+MAGIC = 12582912.0
+BF, F32, I32, U16 = "bfloat16", "float32", "int32", "uint16"
+
+
+def sb(n, d, p=128):
+    return ("sbuf", [p, n], d)
+
+
+SCRATCH = {
+    "pm32": sb(256, I32), "en32": sb(256, I32), "st32": sb(256, I32),
+    "LA": sb(512, U16), "LB": sb(512, U16),
+    "stS": sb(256, BF), "stA": sb(V, BF), "stB": sb(V, BF),
+    "stg": ("dram", [4, 128, 128], U16), "rstg": ("dram", [4, 128, 128], U16),
+    "stg2": ("dram", [4, 128, 64], BF), "rstg2": ("dram", [4, 128, 64], BF),
+    "seed": sb(128, BF), "ones": sb(128, BF), "sel8": sb(8, BF), "sel32": sb(32, BF), "idn": sb(128, BF),
+    "tab": sb(V, BF), "Wb": sb(V, BF), "X": sb(V, BF), "Sc": sb(V, BF), "u": sb(V, BF), "Lb": sb(V, BF),
+    "R4": sb(128, BF), "M64": sb(64, BF), "l1": sb(256, BF), "mf": sb(256, BF),
+    "sb1": sb(256, BF), "land": sb(256, BF), "A1": sb(128, BF),
+    "dL": sb(64, F32), "dT": sb(64, F32), "dH": sb(64, I32), "dF": sb(64, F32), "dQ": sb(64, F32), "dG": sb(64, F32),
+    "vF": sb(64, F32), "rland": ("dram", [4, 128, 64], F32), "oneF": sb(1, F32), "kH": sb(1, F32),
+    "refv": sb(64, F32), "eq": sb(64, F32), "r4": sb(16, F32), "cn": sb(8, F32),
+    "i1": sb(256, I32), "i2": sb(256, I32), "LW": sb(256, U16),
+    "WF": sb(8200, F32), "Yb": sb(V, F32),
+    "psT0": ("psum", [128, 512], F32), "psT1": ("psum", [128, 512], F32), "psT2": ("psum", [128, 512], F32),
+    "psR": ("psum", [128, 1024], BF), "psE0": ("psum", [128, 1024], BF), "psE1": ("psum", [128, 1024], BF),
+    "psE2": ("psum", [128, 1024], BF), "psE3": ("psum", [128, 1024], BF),
+}
+DSEMS = ["d%d" % i for i in range(40)]
+SEMAPHORES = ["qV", "qS", "qP", "qG", "arrL", "arrS", "arrX", "arrF", "arrC", "locL", "locS", "locX", "locF", "locC"] + DSEMS
+
+
+def overlap(a, b):
+    if a[1] >= b[2] or b[1] >= a[2]:
+        return False
+    return a[3] is None or b[3] is None or a[3] == b[3]
+
+
+def reg(r):
+    return r if len(r) == 4 else (r[0], r[1], r[2], None)
+
+
+def add(P, q, fn, rd=(), wr=(), kind="c", sem=None, val=None):
+    i = len(P["ops"])
+    need = set()
+    both = [(reg(r), False) for r in rd] + [(reg(r), True) for r in wr]
+    for r, w in both:
+        ps = r[0].startswith("ps")
+        for (j, r2, w2) in P["acc"].get(r[0], []):
+            o = P["ops"][j]
+            if ps and o["q"] != q:
+                need.add(j)
+            elif (w or w2) and overlap(r, r2):
+                if not (o["q"] == q and o["kind"] == "c" and kind == "c" and not w2):
+                    need.add(j)
+    if q == "G" and kind == "c":
+        need.update(j for j, o in enumerate(P["ops"]) if o["q"] == "G" and o["kind"] == "c")
+    for r, w in both:
+        lst = P["acc"].setdefault(r[0], [])
+        if w and r[3] is None and not r[0].startswith("ps"):
+            lst[:] = [(j, r2, w2) for (j, r2, w2) in lst if not (r[1] <= r2[1] and r2[2] <= r[2] and j in need)]
+        lst.append((i, r, w))
+    P["ops"].append({"q": q, "fn": fn, "kind": kind, "sem": sem, "val": val, "need": need})
+
+
+def emit(P, g, T):
+    eng = {"V": g.vector, "S": g.scalar, "P": g.tensor, "G": g, "Y": g.sync}
+    ops = P["ops"]
+    cnt, know, snap, tot = {}, {}, {}, {}
+    for i, o in enumerate(ops):
+        q = o["q"]
+        k = know.setdefault(q, {})
+        if q == "X":
+            o["at"] = (o["sem"], o["val"])
+            tot[o["sem"]] = o["val"]
+            snap[i] = {}
+            continue
+        for j in sorted(o["need"], reverse=True):
+            s, v = ops[j]["at"]
+            if k.get(s, 0) >= v:
+                continue
+            eng[q].wait_ge(T.sem[s], v)
+            k[s] = v
+            for s2, v2 in snap[j].items():
+                k[s2] = max(k.get(s2, 0), v2)
+        ins = o["fn"](eng[q])
+        if o["kind"] == "c":
+            s = "q" + q
+            cnt[s] = cnt.get(s, 0) + 1
+            o["at"] = (s, cnt[s])
+            ins.then_inc(T.sem[s], 1)
+        else:
+            o["at"] = (o["sem"], o["val"])
+            if o["kind"] == "d":
+                ins.then_inc(T.sem[o["sem"]], 16)
+        tot[o["at"][0]] = o["at"][1]
+        snap[i] = dict(k)
+    for s, v in tot.items():
+        if know["G"].get(s, 0) < v:
+            g.wait_ge(T.sem[s], v)
+
+
+def rank_program(g, core, T, topo):
+    rank = T.rank_of(core)
+    if rank is None:
+        return
+    P = {"ops": [], "acc": {}, "dn": [0]}
+    A, AF = AluOpType, ActivationFunctionType
+    N = len(T.cores)
+    others = [k for k in range(N) if k != rank]
+
+    def full(b):
+        return (b, 0, SCRATCH[b][1][1])
+
+    def vec(fn, rd, wr):
+        add(P, "V", fn, rd, wr)
+
+    def act(out, in_, rd, wr, func=AF.Copy, **kw):
+        add(P, "S", lambda e: e.activation(out, in_, func, **kw), rd, wr)
+
+    def pe(fn, rd, wr):
+        add(P, "P", fn, rd, wr)
+
+    def copy(q, out, in_, rd, wr):
+        if q == "V":
+            vec(lambda e: e.tensor_copy(out, in_), rd, wr)
+        else:
+            act(out, in_, rd, wr)
+
+    def vmin(out, a, b, rd, wr):
+        vec(lambda e: e.tensor_tensor(out, a, b, A.min), rd, wr)
+
+    def zero(q, name, a, b):
+        if q == "V":
+            vec(lambda e: e.memset(T[name][:, a:b], 0.0), [], [(name, a, b)])
+        else:
+            add(P, "G", lambda e: e.iota(T[name][:, a:b], [[0, b - a]], 0, 0, allow_small_or_imprecise_dtypes=True), [], [(name, a, b)])
+
+    def group():
+        P["dn"][0] += 1
+        return DSEMS[P["dn"][0] - 1]
+
+    def dma(out, in_, rd, wr, grp=None, count=1):
+        add(P, "Y", lambda e: e.dma_start(out, in_), rd, wr, kind="d", sem=grp or group(), val=16 * count)
+
+    def gather(q, out, o0, o1, win, lists, l0):
+        a, b = l0 + o0 // 16, l0 + o1 // 16
+        copy(q, T[out][:, o0:o1], T[win][:, 0:V].indirect(T[lists][:, a:b]), [full(win), (lists, a, b)], [(out, o0, o1)])
+
+    def back(q, a, b, lists):
+        gather(q, "u", 128 * a, 128 * b, "Sc", lists, 256)
+
+    def scan(o0, o1, flags):
+        init = 1.0 if o0 == 0 else T.Sc[:, o0 - 1:o0]
+        rd = [(flags, o0, o1), ("X", o0, o1)] + ([("Sc", o0 - 1, o0)] if o0 else [])
+        vec(lambda e: e.tensor_tensor_scan(T.Sc[:, o0:o1], T[flags][:, o0:o1], T.X[:, o0:o1], init, A.max, A.min), rd, [("Sc", o0, o1)])
+
+    def class_minima(win, lists, flags, between=None):
+        for i, (a, b) in enumerate(zip(CUTS, CUTS[1:])):
+            gather("S" if i else "V", "X", a, b, win, lists, 0)
+        if between:
+            between()
+        for a, b in zip(CUTS, CUTS[1:]):
+            scan(a, b, flags)
+
+    def turn(name, a, b, sel, n, step, base):
+        for v in range(a, b):
+            i = v - base
+            o = T[name][:, i:n * step:step] if step else T[name][:, i * n:(i + 1) * n]
+            pe(lambda e, o=o, v=v: e.matmul(o, T.u[:, 128 * v:128 * v + 128], T[sel][:, 0:n], True, True),
+               [("u", 128 * v, 128 * v + 128), full(sel)], [(name, 0, 512, v)] if step else [(name, i * n, (i + 1) * n)])
+
+    def spread(name, a, b):
+        for i, v in enumerate(range(a, b)):
+            pe(lambda e, v=v, i=i: e.transpose(T[name][:, 128 * i:128 * i + 128], T.Lb[:, 128 * v:128 * v + 128], T.idn[:]),
+               [("Lb", 128 * v, 128 * v + 128), full("idn")], [(name, 128 * i, 128 * i + 128)])
+
+    def window_copy(q, name, a, b):
+        n = 128 * (b - a)
+        copy(q, T.Wb[:, 128 * a:128 * b], T[name][:, 0:n], [(name, 0, n)], [("Wb", 128 * a, 128 * b)])
+
+    def min4(bank, n, out, wr):
+        vec(lambda e: e.tensor_tensor_scan(out, T.mf[:, 0:n], T[bank][:, 0:n], 1.0, A.max, A.min), [("mf", 0, n), (bank, 0, 512)], [wr])
+
+    def deal(src):
+        dst = [c for c in T.cores if c != src]
+        off = [c for c in dst if topo.chip(c) != topo.chip(src)]
+        near = [c for c in dst if c not in off]
+        far = topo.engines(src, off[0])
+        rest = [e for e in topo.engines(src, near[0]) if e not in far]
+        out = {}
+        for lst, es in ((off, far), (near, rest)):
+            n = len(es) // len(lst)
+            for i, c in enumerate(lst):
+                out[c] = es[n * i:n * i + n]
+        return out
+
+    NIN = sum(len(deal(T.cores[k])[core]) for k in others)
+
+    def send(parts, sem, loc):
+        es = deal(core)
+        tr, rd = [], []
+        for k in others:
+            c = T.cores[k]
+            src, dst, region = parts(k)
+            rid, pid, _ = topo.addr(c)
+            tr.append(RemoteDMATransfer(dst_ids=[DstId(rid=rid, pnc=pid)], dma_engine_mask=sum(1 << x for x in es[c]),
+                                        remote_sem=T.sem[sem], src=src, dst=dst))
+            rd.append(region)
+        add(P, "G", lambda e: e.remote_dma_fused(tr, local_sem=T.sem[loc]), rd, [], kind="r", sem=loc, val=sum(len(x) for x in es.values()))
+
+    def arrives(sem, wr):
+        add(P, "X", None, [], wr, kind="x", sem=sem, val=NIN)
+
+    dma(T.st32[:], T.st[:], [], [full("st32")])
+    dma(T.pm32[:], T.pm[:], [], [full("pm32")])
+    dma(T.en32[:], T.en[:], [], [full("en32")])
+    add(P, "G", lambda e: e.iota(T.seed[:], [[1, 128]], 128, 0, allow_small_or_imprecise_dtypes=True), [], [full("seed")])
+    vec(lambda e: e.memset(T.ones[:], 1.0), [], [full("ones")])
+    zero("V", "stA", 3200, V)
+    for a in range(0, 1024, 128):
+        vec(lambda e, a=a: e.tensor_scalar(T.tab[:, a:a + 128], T.seed[:], 2.0 ** (a // 128 - 39), None, A.mult), [full("seed")], [("tab", a, a + 128)])
+    for a, b, c in ((1024, 1536, 0), (1536, 2048, 512), (2048, 3072, 0), (3072, V, 1024)):
+        vec(lambda e, a=a, b=b, c=c: e.tensor_scalar(T.tab[:, a:b], T.tab[:, c:c + b - a], 2.0 ** ((a - c) // 128), None, A.mult), [("tab", c, c + b - a)], [("tab", a, b)])
+    for a, b in ((0, 512), (512, 1024), (1024, 1536), (1536, 2176)):
+        act(T.stA[:, a:b], T.tab[:, 0:b - a], [("tab", 0, b - a)], [("stA", a, b)], scale=0.0)
+    zero("G", "stA", 2176, 3200)
+    vec(lambda e: e.tensor_copy(T.stS[:], T.st32[:]), [full("st32")], [full("stS")])
+    vec(lambda e: e.tensor_copy(T.LA[:, 0:256], T.pm32[:]), [full("pm32")], [("LA", 0, 256)])
+    dma(T.stA[OFF:128:16, :], T.stS[:], [full("stS")], [full("stA")])
+    for nm, pat in (("sel8", [[-16, 8]]), ("sel32", [[-64, 2], [0, 4], [-16, 4]]), ("idn", [[-1, 128]])):
+        n = SCRATCH[nm][1][1]
+        base = 0 if nm == "idn" else -OFF
+        add(P, "G", lambda e, nm=nm, pat=pat, n=n, base=base: e.affine_select(T[nm][:], T.ones[:, 0:n], pat, A.is_equal, 0.0, base, 1), [full("ones")], [full(nm)])
+    dma(T.stg2[:], T.stS[:], [full("stS")], [("stg2", 0, 4)])
+    send(lambda k: (T.stg2[k], T.rstg2[rank], ("stg2", k, k + 1)), "arrS", "locS")
+
+    def lists_out():
+        vec(lambda e: e.tensor_copy(T.LA[:, 256:512], T.en32[:]), [full("en32")], [("LA", 256, 512)])
+        dma(T.stg[:], T.LA[:], [full("LA")], [("stg", 0, 4)])
+        send(lambda k: (T.stg[k], T.rstg[rank], ("stg", k, k + 1)), "arrL", "locL")
+
+    class_minima("tab", "LA", "stA", lists_out)
+    for h, h2 in zip(BACK1, BACK1[1:]):
+        back("V", h, h2, "LA")
+        back("S", 16 + h, 16 + h2, "LA")
+        turn("psT0", h, h2, "sel8", 8, 32, 0)
+        turn("psT0", 16 + h, 16 + h2, "sel8", 8, 32, 0)
+    copy("V", T.sb1[:], T.psT0[:, 0:256], [("psT0", 0, 256)], [full("sb1")])
+    own = ("land", 64 * rank, 64 * rank + 64)
+    copy("V", T.land[:, own[1]:own[2]], T.psT0[:, own[1]:own[2]], [("psT0", 0, 256)], [own])
+    send(lambda k: (T.sb1[:, 64 * k:64 * k + 64], T.land[:, own[1]:own[2]], ("sb1", 64 * k, 64 * k + 64)), "arrX", "locX")
+    nA = PARTS["A"][2]
+    zero("G", "Lb", 128 * nA, V)
+    add(P, "G", lambda e: e.iota(T.refv[:], [[128, 32], [0, 2]], int(MAGIC), 1, allow_small_or_imprecise_dtypes=True), [], [full("refv")])
+    zero("G", "WF", 0, 8200)
+    zero("V", "Wb", 2048, V)
+    for nm in ("Wb", "stB"):
+        act(T[nm][:, 0:2048], T.tab[:, 0:2048], [("tab", 0, 2048)], [(nm, 0, 2048)], scale=0.0)
+    zero("V", "stB", 2048, V)
+    zero("V", "mf", 0, 256)
+    vec(lambda e: e.memset(T.mf[:, 0:256:4], 1.0), [], [full("mf")])
+    vec(lambda e: e.memset(T.oneF[:], 1.0), [], [full("oneF")])
+    act(T.kH[:], T.oneF[:], [full("oneF")], [full("kH")], AF.Ln, scale=math.exp(15.5028))
+    arrives("arrS", [("rstg2", k, k + 1) for k in others])
+    arrives("arrL", [("rstg", k, k + 1) for k in others])
+    gl, gs, gw = group(), group(), group()
+    for k in range(N):
+        for grp in range(2):
+            p = 16 * (4 * grp + k)
+            b = "stg" if k == rank else "rstg"
+            dma(T.LB[p:p + 16, :], T[b][k][64 * grp:64 * grp + 64, :], [(b, k, k + 1)], [("LB", 0, 512, p)], gl, 8)
+    for k in range(N):
+        b = "stg2" if k == rank else "rstg2"
+        dma(T.stB[16 * k + OFF:128:64, :], T[b][k], [(b, k, k + 1)], [("stB", 0, V, k)], gs, 4)
+    arrives("arrX", [("land", 64 * k, 64 * k + 64) for k in others])
+    vmin(T.A1[:], T.land[:, 0:128], T.land[:, 128:256], [full("land")], [full("A1")])
+    vmin(T.M64[:], T.A1[:, 0:64], T.A1[:, 64:128], [full("A1")], [full("M64")])
+    pe(lambda e: e.transpose(T.psR[0:64, 0:128], T.M64[:], T.idn[:]), [full("M64"), full("idn")], [("psR", 0, 128)])
+    copy("V", T.R4[0:64, :], T.psR[0:64, 0:128], [("psR", 0, 128)], [full("R4")])
+    for k in range(N):
+        dma(T.Wb[16 * k + OFF:128:64, :], T.R4[0:64, :], [full("R4")], [("Wb", 0, V, k)], gw, 4)
+
+    chunks, free = {}, ["psE0", "psE1", "psE2", "psE3", "psR"]
+    for x in "BCDE":
+        a, m, b = PARTS[x]
+        c = a + WSHARE[x]
+        chunks[x] = [(q, lo, hi, free.pop(0)) for q, lo, hi in (("S", a, c), ("V", c, b)) if hi > lo]
+
+    def part(x, w, q):
+        a, m, b = PARTS[x]
+        if w == "g":
+            back(q, *((a, m) if q == "V" else (m, b)), "LB")
+        elif w == "t":
+            turn(TURN[x], a, b, "sel32", 32, 0, a)
+        elif w == "f":
+            min4(TURN[x], 32 * (b - a), T.Lb[:, 128 * a:128 * b:4], ("Lb", 128 * a, 128 * b))
+        else:
+            for q2, lo, hi, bank in chunks[x]:
+                if w == "e":
+                    spread(bank, lo, hi)
+                elif q2 == q:
+                    window_copy(q, bank, lo, hi)
+
+    def first_part(w, q):
+        b = nA
+        if w == "g":
+            lo, hi = FIRST[q]
+            back(q[0], lo, hi, "LB")
+            for v in range(lo, hi):
+                for grp in range(2):
+                    c = 4 * (b * grp + v)
+                    pe(lambda e, v=v, c=c, h=4 * grp: e.matmul(T.psT0[:, c:c + 4], T.u[:, 128 * v:128 * v + 128], T.sel8[:, h:h + 4], True, True),
+                       [("u", 128 * v, 128 * v + 128), full("sel8")], [("psT0", c, c + 4)])
+        elif w == "f":
+            min4("psT0", 8 * b, T.l1[:, 0:8 * b], ("l1", 0, 8 * b))
+        elif w == "r":
+            pe(lambda e: e.transpose(T.psR[0:2 * b, 0:128], T.l1[:, 3:8 * b:4], T.idn[:]), [("l1", 0, 8 * b), full("idn")], [("psR", 0, 128)])
+        else:
+            copy(q, T.R4[0:2 * b, :], T.psR[0:2 * b, 0:128], [("psR", 0, 128)], [full("R4")])
+            gr = group()
+            for k in range(N):
+                dma(T.Wb[16 * k + OFF:128:64, 0:128 * b], T.R4[0:2 * b, :], [full("R4")], [("Wb", 0, 128 * b, k)], gr, 4)
+
+    for r in range(2, R):
+        class_minima("Wb", "LB", "stB")
+        for x in ORDER.split():
+            if x[0] == "A":
+                first_part(x[1], x[2:])
+            else:
+                part(x[0], x[1], x[2:])
+
+    class_minima("Wb", "LB", "stB")
+    LN2 = math.log(2.0)
+
+    def fold(bank, a, m, b):
+        min4(bank, 8 * (b - a), T.l1[:, 8 * a:8 * b], ("l1", 8 * a, 8 * b))
+
+    for i, (bank, a, m, b) in enumerate(LAST):
+        back("V", a, m, "LB")
+        back("S", m, b, "LB")
+        turn(bank, a, b, "sel8", 8, 0, a)
+        if i:
+            fold(*LAST[i - 1])
+    fold(*LAST[-1])
+    act(T.dL[:], T.l1[:, 3:256:4], [full("l1")], [full("dL")], AF.Ln, scale=65536.0)
+    vec(lambda e: e.tensor_scalar(T.dH[:], T.dL[:], 1.0 / LN2, T.kH[:, 0:1], A.mult, A.add), [full("dL"), full("kH")], [full("dH")])
+    vec(lambda e: e.tensor_scalar(T.dT[:], T.dL[:], 1.0 / LN2, 16.0, A.mult, A.add), [full("dL")], [full("dT")])
+    vec(lambda e: e.tensor_tensor(T.dF[:], T.dT[:], T.dH[:], A.subtract), [full("dT"), full("dH")], [full("dF")])
+    act(T.dQ[:], T.dF[:], [full("dF")], [full("dQ")], AF.Square, scale=6.6406985, bias=6.27066344)
+    vec(lambda e: e.tensor_scalar(T.dG[:], T.dH[:], 128.0, MAGIC - 39.0, A.mult, A.add), [full("dH")], [full("dG")])
+    vec(lambda e: e.tensor_tensor(T.vF[:], T.dQ[:], T.dG[:], A.add), [full("dQ"), full("dG")], [full("vF")])
+    send(lambda k: (T.vF[:], T.rland[rank], full("vF")), "arrF", "locF")
+    dma(T.rland[rank], T.vF[:], [full("vF")], [("rland", rank, rank + 1)])
+    mine = ("r4", 4 * rank, 4 * rank + 2)
+    vec(lambda e: e.tensor_tensor(T.eq[:], T.vF[:], T.refv[:], A.is_equal), [full("vF"), full("refv")], [full("eq")])
+    for i in range(2):
+        c = mine[1] + i
+        vec(lambda e, i=i, c=c: e.tensor_reduce(T.r4[:, c:c + 1], T.eq[:, i:64:2], AxisListType.X, A.add), [full("eq")], [("r4", c, c + 1)])
+    send(lambda k: (T.r4[:, mine[1]:mine[2]], T.r4[:, mine[1]:mine[2]], mine), "arrC", "locC")
+    vec(lambda e: e.tensor_scalar(T.i1[:], T.pm32[:], 7, None, A.arith_shift_right), [full("pm32")], [full("i1")])
+    vec(lambda e: e.tensor_scalar(T.i2[:], T.pm32[:], 64, 1, A.mult, A.add), [full("pm32")], [full("i2")])
+    vec(lambda e: e.tensor_scalar(T.i1[:], T.i1[:], -8190, None, A.mult), [full("i1")], [full("i1")])
+    vec(lambda e: e.tensor_tensor(T.i2[:], T.i1[:], T.i2[:], A.add), [full("i1"), full("i2")], [full("i2")])
+    vec(lambda e: e.tensor_copy(T.LW[:], T.i2[:]), [full("i2")], [full("LW")])
+
+    arrives("arrF", [("rland", k, k + 1) for k in others])
+    gf = group()
+    for i in range(2):
+        dma(T.WF[16 * i:128:32, 1 - i:8193 - i], T.rland[:], [("rland", 0, 4)], [("WF", 0, 8200, i)], gf, 2)
+    arrives("arrC", [("r4", 4 * k, 4 * k + 2) for k in others])
+
+    def final(q, a, b):
+        out, win = T.Yb[:, a:b], T.WF[:, 0:8200].indirect(T.LW[:, a // 16:b // 16])
+        rd, wr = [full("WF"), ("LW", a // 16, b // 16)], [("Yb", a, b)]
+        if q == "V":
+            vec(lambda e: e.tensor_scalar(out, win, -MAGIC, None, A.add), rd, wr)
+        else:
+            act(out, win, rd, wr, AF.Identity, bias=-MAGIC)
+
+    for a, b in ((0, 1024), (1024, 2048)):
+        for q, h in (("V", 0), ("S", 2048)):
+            final(q, h + a, h + b)
+            dma(T.y[:, h + a:h + b], T.Yb[0:128:16, h + a:h + b], [("Yb", h + a, h + b)], [])
+    for i in range(2):
+        pe(lambda e, i=i: e.matmul(T.psT1[0:4, i:i + 1], T.r4[:, i:16:4], T.oneF[:], True, True), [("r4", 4 * k, 4 * k + 2) for k in range(N)] + [full("oneF")], [("psT1", i, i + 1)])
+    vec(lambda e: e.tensor_copy(T.cn[0:4, 0:2], T.psT1[0:4, 0:2]), [("psT1", 0, 2)], [("cn", 0, 2)])
+    dma(T.cnt[:], T.cn[0:4, 0:2], [("cn", 0, 2)], [])
+
+    emit(P, g, T)

@@ -3,14 +3,20 @@ from concourse.mybir import AluOpType, AxisListType, ActivationFunctionType
 import math
 
 V, R = 4096, 6
-PARTS = {"A": (0, 8, 15), "B": (15, 18, 18), "C": (18, 18, 23), "D": (23, 25, 28), "E": (28, 29, 32)}
+PARTS = {"A": (0, 8, 15), "B": (15, 18, 18), "C": (18, 18, 23), "D": (23, 24, 28), "E": (28, 30, 32)}
 FIRST = {"V0": (0, 5), "V1": (5, 8), "S0": (8, 11), "S1": (11, 15)}
 WSHARE = {"B": 3, "C": 5, "D": 0, "E": 2}
 TURN = {"B": "psT1", "C": "psT2", "D": "psT1", "E": "psT2"}
-ORDER = "AgS0 AgV0 AgS1 CgS AgV1 BgV Bt DgV Ct Af Bf Ar DgS Cf Be Dt EgS Ce AwV EgV Df Et Ef De DwV CwS BwS Ee EwS EwV"
-CUTS = [0, 1344, 3328, 4096]
-BACK1 = (0, 7, 13, 16)
-LAST = (("psT0", 0, 8, 17), ("psT1", 17, 22, 28), ("psT2", 28, 30, 32))
+ORDER = "AgS0 AgV0 AgS1 CgS AgV1 DgS BgV DgV Bt Af Ct Bf Cf Ar AwV Be EgV Dt Df EgS BwS Ce Et CwS Ef De Ee EwS DwV EwV"
+PIECES = (("V", 1344), ("S", 3328), ("S", 4096))
+VORDER = "g0 s0 s1 s2"
+CUT1 = (0, 20, 32)
+BACK1 = (("V", 0, 7), ("S", 7, 14), ("V", 14, 17), ("S", 17, 20), ("V", 20, 23), ("S", 23, 28), ("out", 0, "V"), ("V", 28, 30), ("S", 30, 32), ("out", 1, "V"))
+SPREAD1 = (("S", 20, 22), ("V", 22, 26), ("S", 26, 28), ("V", 28, 32))
+LAST = (("psT0", 0, 8, 16), ("psT1", 16, 21, 28), ("psT2", 28, 30, 32))
+ORDER6 = "V0 S0 t0 V1 S1 t1 f0 l0 V2 n0 S2 t2 f1 f2 l1 n1"
+NF = 2
+WF = 64 // NF
 OFF = 12
 MAGIC = 12582912.0
 BF, F32, I32, U16 = "bfloat16", "float32", "int32", "uint16"
@@ -21,26 +27,27 @@ def sb(n, d, p=128):
 
 
 SCRATCH = {
-    "pm32": sb(256, I32), "en32": sb(256, I32), "st32": sb(256, I32),
-    "LA": sb(512, U16), "LB": sb(512, U16),
-    "stS": sb(256, BF), "stA": sb(V, BF), "stB": sb(V, BF),
-    "stg": ("dram", [4, 128, 128], U16), "rstg": ("dram", [4, 128, 128], U16),
-    "stg2": ("dram", [4, 128, 64], BF), "rstg2": ("dram", [4, 128, 64], BF),
-    "seed": sb(128, BF), "ones": sb(128, BF), "sel8": sb(8, BF), "sel32": sb(32, BF), "idn": sb(128, BF),
-    "tab": sb(V, BF), "Wb": sb(V, BF), "X": sb(V, BF), "Sc": sb(V, BF), "u": sb(V, BF), "Lb": sb(V, BF),
-    "R4": sb(128, BF), "M64": sb(64, BF), "l1": sb(256, BF), "mf": sb(256, BF),
-    "sb1": sb(256, BF), "land": sb(256, BF), "A1": sb(128, BF),
-    "dL": sb(64, F32), "dT": sb(64, F32), "dH": sb(64, I32), "dF": sb(64, F32), "dQ": sb(64, F32), "dG": sb(64, F32),
-    "vF": sb(64, F32), "rland": ("dram", [4, 128, 64], F32), "oneF": sb(1, F32), "kH": sb(1, F32),
-    "refv": sb(64, F32), "eq": sb(64, F32), "r4": sb(16, F32), "cn": sb(8, F32),
-    "i1": sb(256, I32), "i2": sb(256, I32), "LW": sb(256, U16),
-    "WF": sb(8200, F32), "Yb": sb(V, F32),
+    "pm32": sb(256, I32), "pmF": sb(256, F32), "Tm": ("sbuf", [128, 8, 32], F32), "st32": ("sbuf", [128, 2, 128], I32),
+    "C1": ("sbuf", [128, 2, 160], BF), "FL": ("sbuf", [128, 2, 160], BF), "O1": ("sbuf", [128, 2, 160], BF),
+    "S1": sb(256, BF), "E1": sb(64, BF), "EF": sb(64, BF), "tri": sb(32, BF), "low": sb(32, BF), "has": sb(2, F32),
+    "sE": ("dram", [4, 128, 64], U16), "rE": ("dram", [4, 128, 64], U16), "sP": ("dram", [4, 128, 64], I32), "rP": ("dram", [4, 128, 64], I32),
+    "sF": ("dram", [4, 128, 64], BF), "rF": ("dram", [4, 128, 64], BF),
+    "en32": sb(256, I32), "LA": sb(256, U16), "sb0": sb(384, BF), "sb1": sb(256, BF), "sb2": sb(256, BF), "A1": sb(128, BF), "M1": sb(64, BF),
+    "PB": sb(256, I32), "LB": sb(512, U16),
+    "stB": sb(V, BF),
+    "ones": sb(128, BF), "sel8": sb(8, BF), "idn": sb(128, BF), "sel32": sb(32, BF),
+    "Wb": sb(V, BF), "X": sb(V, BF), "Sc": sb(V, BF), "u": sb(V, BF), "Lb": sb(V, BF),
+    "R4": sb(128, BF), "l1": sb(256, BF), "mf": sb(256, BF),
+    "dL": sb(64, F32), "vF": sb(64, F32), "rland": ("dram", [NF, 4, 128, 64 // NF], F32),
+    "refv": sb(64, F32), "eq": sb(64, BF), "cn": sb(8, F32), "sC": ("dram", [128, 2], F32), "rC": ("dram", [4, 128, 2], F32),
+    "i1": sb(256, I32), "i2": sb(256, I32), "i3": sb(256, I32), "LW": sb(256, U16),
+    "WF": sb(8208, F32), "Yb": sb(V, F32),
     "psT0": ("psum", [128, 512], F32), "psT1": ("psum", [128, 512], F32), "psT2": ("psum", [128, 512], F32),
     "psR": ("psum", [128, 1024], BF), "psE0": ("psum", [128, 1024], BF), "psE1": ("psum", [128, 1024], BF),
     "psE2": ("psum", [128, 1024], BF), "psE3": ("psum", [128, 1024], BF),
 }
 DSEMS = ["d%d" % i for i in range(40)]
-SEMAPHORES = ["qV", "qS", "qP", "qG", "arrL", "arrS", "arrX", "arrF", "arrC", "locL", "locS", "locX", "locF", "locC"] + DSEMS
+SEMAPHORES = ["qV", "qS", "qP", "qG"] + [a + b for a in ("arr", "loc") for b in ("P", "S", "L", "X0", "X1", "F0", "F1", "C")] + DSEMS
 
 
 def overlap(a, b):
@@ -123,7 +130,7 @@ def rank_program(g, core, T, topo):
     others = [k for k in range(N) if k != rank]
 
     def full(b):
-        return (b, 0, SCRATCH[b][1][1])
+        return (b, 0, math.prod(SCRATCH[b][1][1:]))
 
     def vec(fn, rd, wr):
         add(P, "V", fn, rd, wr)
@@ -140,12 +147,11 @@ def rank_program(g, core, T, topo):
         else:
             act(out, in_, rd, wr)
 
-    def vmin(out, a, b, rd, wr):
-        vec(lambda e: e.tensor_tensor(out, a, b, A.min), rd, wr)
-
     def zero(q, name, a, b):
         if q == "V":
             vec(lambda e: e.memset(T[name][:, a:b], 0.0), [], [(name, a, b)])
+        elif q == "S":
+            act(T[name][:, a:b], T.Wb[:, 0:b - a], [("Wb", 0, b - a)], [(name, a, b)])
         else:
             add(P, "G", lambda e: e.iota(T[name][:, a:b], [[0, b - a]], 0, 0, allow_small_or_imprecise_dtypes=True), [], [(name, a, b)])
 
@@ -153,35 +159,39 @@ def rank_program(g, core, T, topo):
         P["dn"][0] += 1
         return DSEMS[P["dn"][0] - 1]
 
-    def dma(out, in_, rd, wr, grp=None, count=1):
-        add(P, "Y", lambda e: e.dma_start(out, in_), rd, wr, kind="d", sem=grp or group(), val=16 * count)
+    def dma(out, in_, rd, wr, grp=None, count=1, q="Y"):
+        add(P, q, lambda e: e.dma_start(out, in_), rd, wr, kind="d", sem=grp or group(), val=16 * count)
 
-    def gather(q, out, o0, o1, win, lists, l0):
+    def gather(q, out, o0, o1, win, l0, lists="LB"):
         a, b = l0 + o0 // 16, l0 + o1 // 16
         copy(q, T[out][:, o0:o1], T[win][:, 0:V].indirect(T[lists][:, a:b]), [full(win), (lists, a, b)], [(out, o0, o1)])
 
-    def back(q, a, b, lists):
-        gather(q, "u", 128 * a, 128 * b, "Sc", lists, 256)
+    def back(q, a, b):
+        gather(q, "u", 128 * a, 128 * b, "Sc", 256)
 
-    def scan(o0, o1, flags):
+    def scan(o0, o1):
         init = 1.0 if o0 == 0 else T.Sc[:, o0 - 1:o0]
-        rd = [(flags, o0, o1), ("X", o0, o1)] + ([("Sc", o0 - 1, o0)] if o0 else [])
-        vec(lambda e: e.tensor_tensor_scan(T.Sc[:, o0:o1], T[flags][:, o0:o1], T.X[:, o0:o1], init, A.max, A.min), rd, [("Sc", o0, o1)])
+        rd = [("stB", o0, o1), ("X", o0, o1)] + ([("Sc", o0 - 1, o0)] if o0 else [])
+        vec(lambda e: e.tensor_tensor_scan(T.Sc[:, o0:o1], T.stB[:, o0:o1], T.X[:, o0:o1], init, A.max, A.min), rd, [("Sc", o0, o1)])
 
-    def class_minima(win, lists, flags, between=None):
-        for i, (a, b) in enumerate(zip(CUTS, CUTS[1:])):
-            gather("S" if i else "V", "X", a, b, win, lists, 0)
-        if between:
-            between()
-        for a, b in zip(CUTS, CUTS[1:]):
-            scan(a, b, flags)
+    def class_minima():
+        cuts = [0] + [b for q, b in PIECES]
+        for i, (q, b) in enumerate(PIECES):
+            if q == "S":
+                gather(q, "X", cuts[i], b, "Wb", 0)
+        done = 0
+        for x in VORDER.split():
+            i = int(x[1:])
+            if x[0] == "g":
+                gather("V", "X", cuts[i], cuts[i + 1], "Wb", 0)
+            else:
+                scan(done, cuts[i + 1])
+                done = cuts[i + 1]
 
-    def turn(name, a, b, sel, n, step, base):
-        for v in range(a, b):
-            i = v - base
-            o = T[name][:, i:n * step:step] if step else T[name][:, i * n:(i + 1) * n]
-            pe(lambda e, o=o, v=v: e.matmul(o, T.u[:, 128 * v:128 * v + 128], T[sel][:, 0:n], True, True),
-               [("u", 128 * v, 128 * v + 128), full(sel)], [(name, 0, 512, v)] if step else [(name, i * n, (i + 1) * n)])
+    def turn(name, a, b, sel, n):
+        for i, v in enumerate(range(a, b)):
+            pe(lambda e, i=i, v=v: e.matmul(T[name][:, i * n:(i + 1) * n], T.u[:, 128 * v:128 * v + 128], T[sel][:, 0:n], True, True),
+               [("u", 128 * v, 128 * v + 128), full(sel)], [(name, i * n, (i + 1) * n)])
 
     def spread(name, a, b):
         for i, v in enumerate(range(a, b)):
@@ -210,9 +220,9 @@ def rank_program(g, core, T, topo):
 
     NIN = sum(len(deal(T.cores[k])[core]) for k in others)
 
-    def send(parts, sem, loc):
+    def send(parts, sem, loc, after=()):
         es = deal(core)
-        tr, rd = [], []
+        tr, rd = [], list(after)
         for k in others:
             c = T.cores[k]
             src, dst, region = parts(k)
@@ -225,74 +235,134 @@ def rank_program(g, core, T, topo):
     def arrives(sem, wr):
         add(P, "X", None, [], wr, kind="x", sem=sem, val=NIN)
 
-    dma(T.st32[:], T.st[:], [], [full("st32")])
+    def select(out, n, pat, op, base, wr):
+        add(P, "G", lambda e: e.affine_select(out, T.ones[0:out.shape[0], 0:n], pat, op, 0.0, base, 1), [full("ones")], [wr])
+
+    mine = slice(32 * rank, 32 * rank + 32)
+    gs = group()
     dma(T.pm32[:], T.pm[:], [], [full("pm32")])
+    dma(T.sP[:], T.pm[:], [], [("sP", 0, 4)])
+    for i in range(2):
+        dma(T.st32[:, i, :], T.st[i:8:2, :], [], [("st32", 128 * i, 128 * i + 128)], gs, 2)
     dma(T.en32[:], T.en[:], [], [full("en32")])
-    add(P, "G", lambda e: e.iota(T.seed[:], [[1, 128]], 128, 0, allow_small_or_imprecise_dtypes=True), [], [full("seed")])
+    dma(T.rP[rank], T.pm[mine, :], [], [("rP", rank, rank + 1)])
     vec(lambda e: e.memset(T.ones[:], 1.0), [], [full("ones")])
-    zero("V", "stA", 3200, V)
-    for a in range(0, 1024, 128):
-        vec(lambda e, a=a: e.tensor_scalar(T.tab[:, a:a + 128], T.seed[:], 2.0 ** (a // 128 - 39), None, A.mult), [full("seed")], [("tab", a, a + 128)])
-    for a, b, c in ((1024, 1536, 0), (1536, 2048, 512), (2048, 3072, 0), (3072, V, 1024)):
-        vec(lambda e, a=a, b=b, c=c: e.tensor_scalar(T.tab[:, a:b], T.tab[:, c:c + b - a], 2.0 ** ((a - c) // 128), None, A.mult), [("tab", c, c + b - a)], [("tab", a, b)])
-    for a, b in ((0, 512), (512, 1024), (1024, 1536), (1536, 2176)):
-        act(T.stA[:, a:b], T.tab[:, 0:b - a], [("tab", 0, b - a)], [("stA", a, b)], scale=0.0)
-    zero("G", "stA", 2176, 3200)
-    vec(lambda e: e.tensor_copy(T.stS[:], T.st32[:]), [full("st32")], [full("stS")])
-    vec(lambda e: e.tensor_copy(T.LA[:, 0:256], T.pm32[:]), [full("pm32")], [("LA", 0, 256)])
-    dma(T.stA[OFF:128:16, :], T.stS[:], [full("stS")], [full("stA")])
+    act(T.Lb[:, V - 128:V], T.ones[:], [full("ones")], [("Lb", V - 128, V)], AF.Exp)
+    zero("V", "Wb", 0, 1024)
+    zero("V", "Lb", 0, 3072)
+    zero("S", "Lb", 3072, V - 128)
+    for a in range(0, 128, 32):
+        select(T.tri[a:a + 32, :], 32, [[-1, 32]], A.is_ge, 0, ("tri", 0, 32, a))
+    act(T.low[:], T.tri[:], [full("tri")], [full("low")], AF.Identity, scale=-1.0, bias=1.0)
     for nm, pat in (("sel8", [[-16, 8]]), ("sel32", [[-64, 2], [0, 4], [-16, 4]]), ("idn", [[-1, 128]])):
-        n = SCRATCH[nm][1][1]
-        base = 0 if nm == "idn" else -OFF
-        add(P, "G", lambda e, nm=nm, pat=pat, n=n, base=base: e.affine_select(T[nm][:], T.ones[:, 0:n], pat, A.is_equal, 0.0, base, 1), [full("ones")], [full(nm)])
-    dma(T.stg2[:], T.stS[:], [full("stS")], [("stg2", 0, 4)])
-    send(lambda k: (T.stg2[k], T.rstg2[rank], ("stg2", k, k + 1)), "arrS", "locS")
+        select(T[nm][:], SCRATCH[nm][1][1], pat, A.is_equal, 0 if nm == "idn" else -OFF, full(nm))
+    send(lambda k: (T.sP[k], T.rP[rank], ("sP", 0, 4)), "arrP", "locP")
 
-    def lists_out():
-        vec(lambda e: e.tensor_copy(T.LA[:, 256:512], T.en32[:]), [full("en32")], [("LA", 256, 512)])
-        dma(T.stg[:], T.LA[:], [full("LA")], [("stg", 0, 4)])
-        send(lambda k: (T.stg[k], T.rstg[rank], ("stg", k, k + 1)), "arrL", "locL")
-
-    class_minima("tab", "LA", "stA", lists_out)
-    for h, h2 in zip(BACK1, BACK1[1:]):
-        back("V", h, h2, "LA")
-        back("S", 16 + h, 16 + h2, "LA")
-        turn("psT0", h, h2, "sel8", 8, 32, 0)
-        turn("psT0", 16 + h, 16 + h2, "sel8", 8, 32, 0)
-    copy("V", T.sb1[:], T.psT0[:, 0:256], [("psT0", 0, 256)], [full("sb1")])
-    own = ("land", 64 * rank, 64 * rank + 64)
-    copy("V", T.land[:, own[1]:own[2]], T.psT0[:, own[1]:own[2]], [("psT0", 0, 256)], [own])
-    send(lambda k: (T.sb1[:, 64 * k:64 * k + 64], T.land[:, own[1]:own[2]], ("sb1", 64 * k, 64 * k + 64)), "arrX", "locX")
+    vec(lambda e: e.tensor_copy(T.pmF[:], T.pm32[:]), [full("pm32")], [full("pmF")])
+    for c in range(8):
+        vec(lambda e, c=c: e.transpose(T.Tm[:, c, :], T.pmF[:, c:256:8]), [full("pmF")], [("Tm", 32 * c, 32 * c + 32)])
+    for i in range(2):
+        act(T.C1[:, i, 32:160], T.Tm[:, :, 16 * i:16 * i + 16], [full("Tm")], [("C1", 160 * i + 32, 160 * i + 160)], AF.Exp, scale=1.0 / 64, bias=-64.0)
+    vec(lambda e: e.tensor_copy(T.FL[:, :, 32:160], T.st32[:]), [full("st32")], [("FL", 0, 320, "d")])
+    for i in range(2):
+        act(T.O1[:, i, 32:160], T.FL[:, i, 32:160], [("FL", 0, 320, "d")], [("O1", 160 * i, 160 * i + 160), ("has", i, i + 1)], accum_out=T.has[:, i:i + 1])
+    for i in range(2):
+        act(T.EF[:, 32 * i:32 * i + 32], T.low[:], [full("low"), ("has", i, i + 1)], [("EF", 32 * i, 32 * i + 32)], AF.Identity, scale=T.has[:, i:i + 1])
+    for i in range(2):
+        vec(lambda e, i=i: e.tensor_tensor_scan(T.S1[:, 128 * i:128 * i + 128], T.FL[:, i, 32:160], T.C1[:, i, 32:160], 1.0, A.max, A.min),
+            [("FL", 0, 320, "d"), ("C1", 160 * i + 32, 160 * i + 160)], [("S1", 128 * i, 128 * i + 128)])
+    for i in range(2):
+        c = 128 * i + 127
+        vec(lambda e, i=i, c=c: e.tensor_scalar(T.E1[:, 32 * i:32 * i + 32], T.tri[:], T.S1[:, c:c + 1], None, A.max),
+            [full("tri"), ("S1", c, c + 1)], [("E1", 32 * i, 32 * i + 32)])
+    for i in range(2):
+        vec(lambda e, i=i: e.transpose(T.C1[:, i, 0:32], T.E1[:, 32 * i:32 * i + 32]), [("E1", 32 * i, 32 * i + 32)], [("C1", 160 * i, 160 * i + 32)])
+    for i in range(2):
+        vec(lambda e, i=i: e.transpose(T.FL[:, i, 0:32], T.EF[:, 32 * i:32 * i + 32]), [("EF", 32 * i, 32 * i + 32)], [("FL", 0, 320, "t%d" % i)])
+    for i in range(2):
+        vec(lambda e, i=i: e.tensor_tensor_scan(T.O1[:, i, :], T.FL[:, i, :], T.C1[:, i, :], 1.0, A.max, A.min),
+            [full("FL"), ("C1", 160 * i, 160 * i + 160)], [("O1", 160 * i, 160 * i + 160)])
+    gs, go, gr = group(), group(), group()
+    for i in range(2):
+        dma(T.sF[:, 64 * i:64 * i + 64, :], T.FL[:, i, 32:160], [("FL", 0, 320, "d")], [("sF", 0, 4, i)], gs, 2)
+        dma(T.rF[rank, 64 * i:64 * i + 64, :], T.FL[mine, i, 32:160], [("FL", 0, 320, "d")], [("rF", rank, rank + 1, i)], go, 2)
+    for i in range(2):
+        dma(T.Lb[16 * i + OFF:128:32, :], T.O1[:, i, 32:160], [("O1", 160 * i, 160 * i + 160)], [("Lb", 0, V, i)], gr, 2)
+    send(lambda k: (T.sF[k], T.rF[rank], ("sF", 0, 4)), "arrS", "locS")
+    vec(lambda e: e.tensor_copy(T.LA[:], T.en32[:]), [full("en32")], [full("LA")])
+    dma(T.sE[:], T.LA[:], [full("LA")], [("sE", 0, 4)])
+    dma(T.rE[rank], T.LA[mine, :], [full("LA")], [("rE", rank, rank + 1)])
     nA = PARTS["A"][2]
-    zero("G", "Lb", 128 * nA, V)
-    add(P, "G", lambda e: e.iota(T.refv[:], [[128, 32], [0, 2]], int(MAGIC), 1, allow_small_or_imprecise_dtypes=True), [], [full("refv")])
-    zero("G", "WF", 0, 8200)
-    zero("V", "Wb", 2048, V)
-    for nm in ("Wb", "stB"):
-        act(T[nm][:, 0:2048], T.tab[:, 0:2048], [("tab", 0, 2048)], [(nm, 0, 2048)], scale=0.0)
-    zero("V", "stB", 2048, V)
+    act(T.Wb[:, 1024:1152], T.ones[:], [full("ones")], [("Wb", 1024, 1152)], AF.Ln)
+    zero("V", "Wb", 1152, 128 * max(nA, CUT1[1]))
     zero("V", "mf", 0, 256)
     vec(lambda e: e.memset(T.mf[:, 0:256:4], 1.0), [], [full("mf")])
-    vec(lambda e: e.memset(T.oneF[:], 1.0), [], [full("oneF")])
-    act(T.kH[:], T.oneF[:], [full("oneF")], [full("kH")], AF.Ln, scale=math.exp(15.5028))
-    arrives("arrS", [("rstg2", k, k + 1) for k in others])
-    arrives("arrL", [("rstg", k, k + 1) for k in others])
-    gl, gs, gw = group(), group(), group()
-    for k in range(N):
+
+    def fetch(sem, src, dst, cols, rows=False):
+        arrives(sem, [(src, k, k + 1) for k in others])
+        gl, h = group(), SCRATCH[src][1][1] // 2
         for grp in range(2):
-            p = 16 * (4 * grp + k)
-            b = "stg" if k == rank else "rstg"
-            dma(T.LB[p:p + 16, :], T[b][k][64 * grp:64 * grp + 64, :], [(b, k, k + 1)], [("LB", 0, 512, p)], gl, 8)
+            out = T[dst][64 * grp + OFF:64 * grp + 64:16, :] if rows else T[dst][64 * grp:64 * grp + 64, cols[0]:cols[1]]
+            dma(out, T[src][:, h * grp:h * grp + h, :], [(src, 0, 4)], [(dst,) + cols + (grp,)], gl, 2)
+
+    fetch("arrP", "rP", "PB", (0, 256))
+    H = CUT1[1]
+
+    def out1(j, q):
+        bank, name, w = "psT%d" % j, "sb%d" % j, 2 * (CUT1[j + 1] - CUT1[j])
+        copy(q, T[name][:, 0:4 * w], T[bank][:, 0:4 * w], [(bank, 0, 512)], [(name, 0, 4 * w)])
+        own = (name, (4 + rank) * w, (5 + rank) * w)
+        send(lambda k: (T[name][:, w * k:w * k + w], T[name][:, own[1]:own[2]], (name, w * k, w * k + w)), "arrX%d" % j, "locX%d" % j)
+
+    def in1(j):
+        name, w = "sb%d" % j, 2 * (CUT1[j + 1] - CUT1[j])
+        arrives("arrX%d" % j, [(name, (4 + k) * w, (5 + k) * w) for k in others])
+        vec(lambda e: e.tensor_tensor(T.A1[:, 0:2 * w], T[name][:, 4 * w:6 * w], T[name][:, 6 * w:8 * w], A.min), [(name, 4 * w, 8 * w)], [full("A1")])
+        return w
+
+    def turn1(v):
+        j = max(i for i, c in enumerate(CUT1) if c <= v)
+        bank, n, rd = "psT%d" % j, CUT1[j + 1] - CUT1[j], [("stB", 128 * v, 128 * v + 128), full("sel8")]
+        if j == 0:
+            pe(lambda e: e.matmul(T[bank][:, v:8 * n:n], T.stB[:, 128 * v:128 * v + 128], T.sel8[:], True, True), rd, [(bank, 0, 512, v)])
+        else:
+            for i in range(2):
+                c = 2 * (v - CUT1[j]) + i
+                pe(lambda e, c=c, i=i: e.matmul(T[bank][:, c:8 * n:2 * n], T.stB[:, 128 * v:128 * v + 128], T.sel8[:, i:8:2], True, True), rd, [(bank, 0, 512, c)])
+
+    for x in BACK1:
+        if x[0] == "out":
+            out1(x[1], x[2])
+        else:
+            gather(x[0], "stB", 128 * x[1], 128 * x[2], "Lb", 0, "LA")
+            for v in range(x[1], x[2]):
+                turn1(v)
+    send(lambda k: (T.sE[k], T.rE[rank], ("sE", 0, 4)), "arrL", "locL")
+    for j in range(len(CUT1) - 1):
+        name, w = "sb%d" % j, 2 * (CUT1[j + 1] - CUT1[j])
+        copy("S", T[name][:, (4 + rank) * w:(5 + rank) * w], T[name][:, w * rank:w * rank + w], [(name, w * rank, w * rank + w)], [(name, (4 + rank) * w, (5 + rank) * w)])
+    vec(lambda e: e.tensor_copy(T.LB[:, 0:256], T.PB[:]), [full("PB")], [("LB", 0, 256)])
+    fetch("arrS", "rF", "stB", (0, V), True)
+    add(P, "G", lambda e: e.iota(T.refv[:], [[128, 32], [0, 2]], int(MAGIC), 1, allow_small_or_imprecise_dtypes=True), [], [full("refv")])
+    zero("G", "WF", 0, 8208)
+    in1(0)
+    vec(lambda e: e.tensor_tensor(T.M1[:, 0:2 * H], T.A1[:, 0:2 * H], T.A1[:, 2 * H:4 * H], A.min), [full("A1")], [full("M1")])
+    pe(lambda e: e.transpose(T.psR[0:2 * H, 0:128], T.M1[:, 0:2 * H], T.idn[:]), [full("M1"), full("idn")], [("psR", 0, 128)])
+    copy("V", T.R4[0:2 * H, :], T.psR[0:2 * H, 0:128], [("psR", 0, 128)], [full("R4")])
+    gr = group()
     for k in range(N):
-        b = "stg2" if k == rank else "rstg2"
-        dma(T.stB[16 * k + OFF:128:64, :], T[b][k], [(b, k, k + 1)], [("stB", 0, V, k)], gs, 4)
-    arrives("arrX", [("land", 64 * k, 64 * k + 64) for k in others])
-    vmin(T.A1[:], T.land[:, 0:128], T.land[:, 128:256], [full("land")], [full("A1")])
-    vmin(T.M64[:], T.A1[:, 0:64], T.A1[:, 64:128], [full("A1")], [full("M64")])
-    pe(lambda e: e.transpose(T.psR[0:64, 0:128], T.M64[:], T.idn[:]), [full("M64"), full("idn")], [("psR", 0, 128)])
-    copy("V", T.R4[0:64, :], T.psR[0:64, 0:128], [("psR", 0, 128)], [full("R4")])
-    for k in range(N):
-        dma(T.Wb[16 * k + OFF:128:64, :], T.R4[0:64, :], [full("R4")], [("Wb", 0, V, k)], gw, 4)
+        dma(T.Wb[16 * k + OFF:128:64, 0:128 * H], T.R4[0:2 * H, :], [full("R4")], [("Wb", 0, 128 * H, k)], gr, 4)
+    fetch("arrL", "rE", "LB", (256, 512))
+    dma(T.sC[:], T.refv[:, 0:2], [full("refv")], [("sC", 0, 1)])
+    for j in range(1, len(CUT1) - 1):
+        w, a, b = in1(j), 128 * CUT1[j], 128 * CUT1[j + 1]
+        for k in range(N):
+            vec(lambda e, k=k, w=w, a=a, b=b: e.tensor_tensor(T.Lb[:, a + 16 * k + OFF:b:64], T.A1[:, 0:w], T.A1[:, w:2 * w], A.min), [full("A1")], [("Lb", a, b, k)])
+        mine1 = [(i, x) for i, x in enumerate(SPREAD1) if a <= 128 * x[1] < b]
+        for i, (q, lo, hi) in mine1:
+            spread("psE%d" % i, lo, hi)
+        for i, (q, lo, hi) in mine1:
+            window_copy(q, "psE%d" % i, lo, hi)
 
     chunks, free = {}, ["psE0", "psE1", "psE2", "psE3", "psR"]
     for x in "BCDE":
@@ -303,9 +373,9 @@ def rank_program(g, core, T, topo):
     def part(x, w, q):
         a, m, b = PARTS[x]
         if w == "g":
-            back(q, *((a, m) if q == "V" else (m, b)), "LB")
+            back(q, *((a, m) if q == "V" else (m, b)))
         elif w == "t":
-            turn(TURN[x], a, b, "sel32", 32, 0, a)
+            turn(TURN[x], a, b, "sel32", 32)
         elif w == "f":
             min4(TURN[x], 32 * (b - a), T.Lb[:, 128 * a:128 * b:4], ("Lb", 128 * a, 128 * b))
         else:
@@ -319,7 +389,7 @@ def rank_program(g, core, T, topo):
         b = nA
         if w == "g":
             lo, hi = FIRST[q]
-            back(q[0], lo, hi, "LB")
+            back(q[0], lo, hi)
             for v in range(lo, hi):
                 for grp in range(2):
                     c = 4 * (b * grp + v)
@@ -336,55 +406,66 @@ def rank_program(g, core, T, topo):
                 dma(T.Wb[16 * k + OFF:128:64, 0:128 * b], T.R4[0:2 * b, :], [full("R4")], [("Wb", 0, 128 * b, k)], gr, 4)
 
     for r in range(2, R):
-        class_minima("Wb", "LB", "stB")
+        class_minima()
         for x in ORDER.split():
             if x[0] == "A":
                 first_part(x[1], x[2:])
             else:
                 part(x[0], x[1], x[2:])
-
-    class_minima("Wb", "LB", "stB")
-    LN2 = math.log(2.0)
+    class_minima()
 
     def fold(bank, a, m, b):
         min4(bank, 8 * (b - a), T.l1[:, 8 * a:8 * b], ("l1", 8 * a, 8 * b))
 
-    for i, (bank, a, m, b) in enumerate(LAST):
-        back("V", a, m, "LB")
-        back("S", m, b, "LB")
-        turn(bank, a, b, "sel8", 8, 0, a)
-        if i:
-            fold(*LAST[i - 1])
-    fold(*LAST[-1])
-    act(T.dL[:], T.l1[:, 3:256:4], [full("l1")], [full("dL")], AF.Ln, scale=65536.0)
-    vec(lambda e: e.tensor_scalar(T.dH[:], T.dL[:], 1.0 / LN2, T.kH[:, 0:1], A.mult, A.add), [full("dL"), full("kH")], [full("dH")])
-    vec(lambda e: e.tensor_scalar(T.dT[:], T.dL[:], 1.0 / LN2, 16.0, A.mult, A.add), [full("dL")], [full("dT")])
-    vec(lambda e: e.tensor_tensor(T.dF[:], T.dT[:], T.dH[:], A.subtract), [full("dT"), full("dH")], [full("dF")])
-    act(T.dQ[:], T.dF[:], [full("dF")], [full("dQ")], AF.Square, scale=6.6406985, bias=6.27066344)
-    vec(lambda e: e.tensor_scalar(T.dG[:], T.dH[:], 128.0, MAGIC - 39.0, A.mult, A.add), [full("dH")], [full("dG")])
-    vec(lambda e: e.tensor_tensor(T.vF[:], T.dQ[:], T.dG[:], A.add), [full("dQ"), full("dG")], [full("vF")])
-    send(lambda k: (T.vF[:], T.rland[rank], full("vF")), "arrF", "locF")
-    dma(T.rland[rank], T.vF[:], [full("vF")], [("rland", rank, rank + 1)])
-    mine = ("r4", 4 * rank, 4 * rank + 2)
+    def logs(h):
+        a, b = WF * h, WF * h + WF
+        act(T.dL[:, a:b], T.l1[:, 4 * a + 3:4 * b:4], [("l1", 4 * a, 4 * b)], [("dL", a, b)], AF.Ln, scale=math.exp(32.0))
+
+    def numbers(h):
+        part = ("vF", WF * h, WF * h + WF)
+        vec(lambda e: e.tensor_scalar(T.vF[:, part[1]:part[2]], T.dL[:, part[1]:part[2]], 64.0, MAGIC + 2048.0, A.mult, A.add), [("dL", part[1], part[2])], [part])
+        send(lambda k: (T.vF[:, part[1]:part[2]], T.rland[h, rank], part), "arrF%d" % h, "locF%d" % h)
+        dma(T.rland[h, rank], T.vF[:, part[1]:part[2]], [part], [("rland", 4 * h + rank, 4 * h + rank + 1)])
+
+    for x in ORDER6.split():
+        i = int(x[1])
+        bank, a, m, b = LAST[i]
+        if x[0] == "V":
+            back("V", a, m)
+        elif x[0] == "S":
+            back("S", m, b)
+        elif x[0] == "t":
+            turn(bank, a, b, "sel8", 8)
+        elif x[0] == "f":
+            fold(bank, a, m, b)
+        elif x[0] == "l":
+            logs(i)
+        else:
+            numbers(i)
     vec(lambda e: e.tensor_tensor(T.eq[:], T.vF[:], T.refv[:], A.is_equal), [full("vF"), full("refv")], [full("eq")])
+    pe(lambda e: e.matmul(T.psT1[0:1, 0:64], T.ones[:, 0:1], T.eq[:], True, True), [full("eq"), full("ones")], [("psT1", 0, 64)])
     for i in range(2):
-        c = mine[1] + i
-        vec(lambda e, i=i, c=c: e.tensor_reduce(T.r4[:, c:c + 1], T.eq[:, i:64:2], AxisListType.X, A.add), [full("eq")], [("r4", c, c + 1)])
-    send(lambda k: (T.r4[:, mine[1]:mine[2]], T.r4[:, mine[1]:mine[2]], mine), "arrC", "locC")
+        act(T.dL[0:1, 0:32], T.psT1[0:1, i:64:2], [("psT1", 0, 64)], [("dL", 0, 32), ("cn", i, i + 1)], accum_out=T.cn[0:1, i:i + 1])
+    dma(T.sC[0:1, :], T.cn[0:1, 0:2], [("cn", 0, 2)], [("sC", 0, 1)])
+    dma(T.rC[rank, 0:1, :], T.cn[0:1, 0:2], [("cn", 0, 2)], [("rC", rank, rank + 1)])
+    send(lambda k: (T.sC[:], T.rC[rank], ("sC", 0, 1)), "arrC", "locC")
     vec(lambda e: e.tensor_scalar(T.i1[:], T.pm32[:], 7, None, A.arith_shift_right), [full("pm32")], [full("i1")])
-    vec(lambda e: e.tensor_scalar(T.i2[:], T.pm32[:], 64, 1, A.mult, A.add), [full("pm32")], [full("i2")])
-    vec(lambda e: e.tensor_scalar(T.i1[:], T.i1[:], -8190, None, A.mult), [full("i1")], [full("i1")])
-    vec(lambda e: e.tensor_tensor(T.i2[:], T.i1[:], T.i2[:], A.add), [full("i1"), full("i2")], [full("i2")])
+    vec(lambda e: e.tensor_scalar(T.i2[:], T.pm32[:], WF, 1, A.mult, A.add), [full("pm32")], [full("i2")])
+    if NF == 2:
+        vec(lambda e: e.tensor_scalar(T.i3[:], T.pm32[:], 2048, 4072, A.is_ge, A.mult), [full("pm32")], [full("i3")])
+    vec(lambda e: e.tensor_scalar(T.i1[:], T.i1[:], 2 - 128 * WF, None, A.mult), [full("i1")], [full("i1")])
+    for a in ("i1", "i3")[:NF]:
+        vec(lambda e, a=a: e.tensor_tensor(T.i2[:], T[a][:], T.i2[:], A.add), [full(a), full("i2")], [full("i2")])
     vec(lambda e: e.tensor_copy(T.LW[:], T.i2[:]), [full("i2")], [full("LW")])
 
-    arrives("arrF", [("rland", k, k + 1) for k in others])
-    gf = group()
-    for i in range(2):
-        dma(T.WF[16 * i:128:32, 1 - i:8193 - i], T.rland[:], [("rland", 0, 4)], [("WF", 0, 8200, i)], gf, 2)
-    arrives("arrC", [("r4", 4 * k, 4 * k + 2) for k in others])
+    for h in range(NF):
+        arrives("arrF%d" % h, [("rland", 4 * h + k, 4 * h + k + 1) for k in others])
+        gf, c = group(), 4104 * h + 1
+        for i in range(2):
+            dma(T.WF[16 * i:128:32, c - i:c + 128 * WF - i], T.rland[h], [("rland", 4 * h, 4 * h + 4)], [("WF", c - 1, c + 128 * WF, i)], gf, 2)
 
     def final(q, a, b):
-        out, win = T.Yb[:, a:b], T.WF[:, 0:8200].indirect(T.LW[:, a // 16:b // 16])
+        out, win = T.Yb[:, a:b], T.WF[:, 0:8208].indirect(T.LW[:, a // 16:b // 16])
         rd, wr = [full("WF"), ("LW", a // 16, b // 16)], [("Yb", a, b)]
         if q == "V":
             vec(lambda e: e.tensor_scalar(out, win, -MAGIC, None, A.add), rd, wr)
@@ -395,9 +476,7 @@ def rank_program(g, core, T, topo):
         for q, h in (("V", 0), ("S", 2048)):
             final(q, h + a, h + b)
             dma(T.y[:, h + a:h + b], T.Yb[0:128:16, h + a:h + b], [("Yb", h + a, h + b)], [])
-    for i in range(2):
-        pe(lambda e, i=i: e.matmul(T.psT1[0:4, i:i + 1], T.r4[:, i:16:4], T.oneF[:], True, True), [("r4", 4 * k, 4 * k + 2) for k in range(N)] + [full("oneF")], [("psT1", i, i + 1)])
-    vec(lambda e: e.tensor_copy(T.cn[0:4, 0:2], T.psT1[0:4, 0:2]), [("psT1", 0, 2)], [("cn", 0, 2)])
-    dma(T.cnt[:], T.cn[0:4, 0:2], [("cn", 0, 2)], [])
+    arrives("arrC", [("rC", k, k + 1) for k in others])
+    dma(T.cnt[:], T.rC[:, 0, :], [("rC", 0, 4)], [], q="S")
 
     emit(P, g, T)

from concourse.bass import DstId, RemoteDMATransfer
from concourse.mybir import AluOpType, AxisListType, ActivationFunctionType
import math

V, R = 4096, 6
PARTS = {"A": (0, 8, 15), "B": (15, 18, 18), "C": (18, 18, 23), "D": (23, 24, 28), "E": (28, 30, 32)}
FIRST = {"V0": (0, 5), "V1": (5, 8), "S0": (8, 11), "S1": (11, 15)}
WSHARE = {"B": 3, "C": 5, "D": 0, "E": 2}
TURN = {"B": "psT1", "C": "psT2", "D": "psT1", "E": "psT2"}
ORDER = "AgS0 AgV0 AgS1 CgS AgV1 DgS BgV DgV Bt Af Ct Bf Cf Ar AwV Be EgV Dt Df EgS BwS Ce Et CwS Ef De Ee EwS DwV EwV"
PIECES = (("V", 1344), ("S", 3328), ("S", 4096))
VORDER = "g0 s0 s1 s2"
CUT1 = (0, 20, 32)
BACK1 = (("V", 0, 7), ("S", 7, 14), ("V", 14, 17), ("S", 17, 20), ("V", 20, 23), ("S", 23, 28), ("out", 0, "V"), ("V", 28, 30), ("S", 30, 32), ("out", 1, "V"))
SPREAD1 = (("S", 20, 22), ("V", 22, 26), ("S", 26, 28), ("V", 28, 32))
LAST = (("psT0", 0, 8, 16), ("psT1", 16, 21, 28), ("psT2", 28, 30, 32))
ORDER6 = "V0 S0 t0 V1 S1 t1 f0 l0 V2 n0 S2 t2 f1 f2 l1 n1"
NF = 2
WF = 64 // NF
OFF = 12
MAGIC = 12582912.0
BF, F32, I32, U16 = "bfloat16", "float32", "int32", "uint16"


def sb(n, d, p=128):
    return ("sbuf", [p, n], d)


SCRATCH = {
    "pm32": sb(256, I32), "pmF": sb(256, F32), "Tm": ("sbuf", [128, 8, 32], F32), "st32": ("sbuf", [128, 2, 128], I32),
    "C1": ("sbuf", [128, 2, 160], BF), "FL": ("sbuf", [128, 2, 160], BF), "O1": ("sbuf", [128, 2, 160], BF),
    "S1": sb(256, BF), "E1": sb(64, BF), "EF": sb(64, BF), "tri": sb(32, BF), "low": sb(32, BF), "has": sb(2, F32),
    "sE": ("dram", [4, 128, 64], U16), "rE": ("dram", [4, 128, 64], U16), "sP": ("dram", [4, 128, 64], I32), "rP": ("dram", [4, 128, 64], I32),
    "sF": ("dram", [4, 128, 64], BF), "rF": ("dram", [4, 128, 64], BF),
    "en32": sb(256, I32), "LA": sb(256, U16), "sb0": sb(384, BF), "sb1": sb(256, BF), "sb2": sb(256, BF), "A1": sb(128, BF), "M1": sb(64, BF),
    "PB": sb(256, I32), "LB": sb(512, U16),
    "stB": sb(V, BF),
    "ones": sb(128, BF), "sel8": sb(8, BF), "idn": sb(128, BF), "sel32": sb(32, BF),
    "Wb": sb(V, BF), "X": sb(V, BF), "Sc": sb(V, BF), "u": sb(V, BF), "Lb": sb(V, BF),
    "R4": sb(128, BF), "l1": sb(256, BF), "mf": sb(256, BF),
    "dL": sb(64, F32), "vF": sb(64, F32), "rland": ("dram", [NF, 4, 128, 64 // NF], F32),
    "refv": sb(64, F32), "eq": sb(64, BF), "cn": sb(8, F32), "sC": ("dram", [128, 2], F32), "rC": ("dram", [4, 128, 2], F32),
    "i1": sb(256, I32), "i2": sb(256, I32), "i3": sb(256, I32), "LW": sb(256, U16),
    "WF": sb(8208, F32), "Yb": sb(V, F32),
    "psT0": ("psum", [128, 512], F32), "psT1": ("psum", [128, 512], F32), "psT2": ("psum", [128, 512], F32),
    "psR": ("psum", [128, 1024], BF), "psE0": ("psum", [128, 1024], BF), "psE1": ("psum", [128, 1024], BF),
    "psE2": ("psum", [128, 1024], BF), "psE3": ("psum", [128, 1024], BF),
}
DSEMS = ["d%d" % i for i in range(40)]
SEMAPHORES = ["qV", "qS", "qP", "qG"] + [a + b for a in ("arr", "loc") for b in ("P", "S", "L", "X0", "X1", "F0", "F1", "C")] + DSEMS


def overlap(a, b):
    if a[1] >= b[2] or b[1] >= a[2]:
        return False
    return a[3] is None or b[3] is None or a[3] == b[3]


def reg(r):
    return r if len(r) == 4 else (r[0], r[1], r[2], None)


def add(P, q, fn, rd=(), wr=(), kind="c", sem=None, val=None):
    i = len(P["ops"])
    need = set()
    both = [(reg(r), False) for r in rd] + [(reg(r), True) for r in wr]
    for r, w in both:
        ps = r[0].startswith("ps")
        for (j, r2, w2) in P["acc"].get(r[0], []):
            o = P["ops"][j]
            if ps and o["q"] != q:
                need.add(j)
            elif (w or w2) and overlap(r, r2):
                if not (o["q"] == q and o["kind"] == "c" and kind == "c" and not w2):
                    need.add(j)
    if q == "G" and kind == "c":
        need.update(j for j, o in enumerate(P["ops"]) if o["q"] == "G" and o["kind"] == "c")
    for r, w in both:
        lst = P["acc"].setdefault(r[0], [])
        if w and r[3] is None and not r[0].startswith("ps"):
            lst[:] = [(j, r2, w2) for (j, r2, w2) in lst if not (r[1] <= r2[1] and r2[2] <= r[2] and j in need)]
        lst.append((i, r, w))
    P["ops"].append({"q": q, "fn": fn, "kind": kind, "sem": sem, "val": val, "need": need})


def emit(P, g, T):
    eng = {"V": g.vector, "S": g.scalar, "P": g.tensor, "G": g, "Y": g.sync}
    ops = P["ops"]
    cnt, know, snap, tot = {}, {}, {}, {}
    for i, o in enumerate(ops):
        q = o["q"]
        k = know.setdefault(q, {})
        if q == "X":
            o["at"] = (o["sem"], o["val"])
            tot[o["sem"]] = o["val"]
            snap[i] = {}
            continue
        for j in sorted(o["need"], reverse=True):
            s, v = ops[j]["at"]
            if k.get(s, 0) >= v:
                continue
            eng[q].wait_ge(T.sem[s], v)
            k[s] = v
            for s2, v2 in snap[j].items():
                k[s2] = max(k.get(s2, 0), v2)
        ins = o["fn"](eng[q])
        if o["kind"] == "c":
            s = "q" + q
            cnt[s] = cnt.get(s, 0) + 1
            o["at"] = (s, cnt[s])
            ins.then_inc(T.sem[s], 1)
        else:
            o["at"] = (o["sem"], o["val"])
            if o["kind"] == "d":
                ins.then_inc(T.sem[o["sem"]], 16)
        tot[o["at"][0]] = o["at"][1]
        snap[i] = dict(k)
    for s, v in tot.items():
        if know["G"].get(s, 0) < v:
            g.wait_ge(T.sem[s], v)


def rank_program(g, core, T, topo):
    rank = T.rank_of(core)
    if rank is None:
        return
    P = {"ops": [], "acc": {}, "dn": [0]}
    A, AF = AluOpType, ActivationFunctionType
    N = len(T.cores)
    others = [k for k in range(N) if k != rank]

    def full(b):
        return (b, 0, math.prod(SCRATCH[b][1][1:]))

    def vec(fn, rd, wr):
        add(P, "V", fn, rd, wr)

    def act(out, in_, rd, wr, func=AF.Copy, **kw):
        add(P, "S", lambda e: e.activation(out, in_, func, **kw), rd, wr)

    def pe(fn, rd, wr):
        add(P, "P", fn, rd, wr)

    def copy(q, out, in_, rd, wr):
        if q == "V":
            vec(lambda e: e.tensor_copy(out, in_), rd, wr)
        else:
            act(out, in_, rd, wr)

    def zero(q, name, a, b):
        if q == "V":
            vec(lambda e: e.memset(T[name][:, a:b], 0.0), [], [(name, a, b)])
        elif q == "S":
            act(T[name][:, a:b], T.Wb[:, 0:b - a], [("Wb", 0, b - a)], [(name, a, b)])
        else:
            add(P, "G", lambda e: e.iota(T[name][:, a:b], [[0, b - a]], 0, 0, allow_small_or_imprecise_dtypes=True), [], [(name, a, b)])

    def group():
        P["dn"][0] += 1
        return DSEMS[P["dn"][0] - 1]

    def dma(out, in_, rd, wr, grp=None, count=1, q="Y"):
        add(P, q, lambda e: e.dma_start(out, in_), rd, wr, kind="d", sem=grp or group(), val=16 * count)

    def gather(q, out, o0, o1, win, l0, lists="LB"):
        a, b = l0 + o0 // 16, l0 + o1 // 16
        copy(q, T[out][:, o0:o1], T[win][:, 0:V].indirect(T[lists][:, a:b]), [full(win), (lists, a, b)], [(out, o0, o1)])

    def back(q, a, b):
        gather(q, "u", 128 * a, 128 * b, "Sc", 256)

    def scan(o0, o1):
        init = 1.0 if o0 == 0 else T.Sc[:, o0 - 1:o0]
        rd = [("stB", o0, o1), ("X", o0, o1)] + ([("Sc", o0 - 1, o0)] if o0 else [])
        vec(lambda e: e.tensor_tensor_scan(T.Sc[:, o0:o1], T.stB[:, o0:o1], T.X[:, o0:o1], init, A.max, A.min), rd, [("Sc", o0, o1)])

    def class_minima():
        cuts = [0] + [b for q, b in PIECES]
        for i, (q, b) in enumerate(PIECES):
            if q == "S":
                gather(q, "X", cuts[i], b, "Wb", 0)
        done = 0
        for x in VORDER.split():
            i = int(x[1:])
            if x[0] == "g":
                gather("V", "X", cuts[i], cuts[i + 1], "Wb", 0)
            else:
                scan(done, cuts[i + 1])
                done = cuts[i + 1]

    def turn(name, a, b, sel, n):
        for i, v in enumerate(range(a, b)):
            pe(lambda e, i=i, v=v: e.matmul(T[name][:, i * n:(i + 1) * n], T.u[:, 128 * v:128 * v + 128], T[sel][:, 0:n], True, True),
               [("u", 128 * v, 128 * v + 128), full(sel)], [(name, i * n, (i + 1) * n)])

    def spread(name, a, b):
        for i, v in enumerate(range(a, b)):
            pe(lambda e, v=v, i=i: e.transpose(T[name][:, 128 * i:128 * i + 128], T.Lb[:, 128 * v:128 * v + 128], T.idn[:]),
               [("Lb", 128 * v, 128 * v + 128), full("idn")], [(name, 128 * i, 128 * i + 128)])

    def window_copy(q, name, a, b):
        n = 128 * (b - a)
        copy(q, T.Wb[:, 128 * a:128 * b], T[name][:, 0:n], [(name, 0, n)], [("Wb", 128 * a, 128 * b)])

    def min4(bank, n, out, wr):
        vec(lambda e: e.tensor_tensor_scan(out, T.mf[:, 0:n], T[bank][:, 0:n], 1.0, A.max, A.min), [("mf", 0, n), (bank, 0, 512)], [wr])

    def deal(src):
        dst = [c for c in T.cores if c != src]
        off = [c for c in dst if topo.chip(c) != topo.chip(src)]
        near = [c for c in dst if c not in off]
        far = topo.engines(src, off[0])
        rest = [e for e in topo.engines(src, near[0]) if e not in far]
        out = {}
        for lst, es in ((off, far), (near, rest)):
            n = len(es) // len(lst)
            for i, c in enumerate(lst):
                out[c] = es[n * i:n * i + n]
        return out

    NIN = sum(len(deal(T.cores[k])[core]) for k in others)

    def send(parts, sem, loc, after=()):
        es = deal(core)
        tr, rd = [], list(after)
        for k in others:
            c = T.cores[k]
            src, dst, region = parts(k)
            rid, pid, _ = topo.addr(c)
            tr.append(RemoteDMATransfer(dst_ids=[DstId(rid=rid, pnc=pid)], dma_engine_mask=sum(1 << x for x in es[c]),
                                        remote_sem=T.sem[sem], src=src, dst=dst))
            rd.append(region)
        add(P, "G", lambda e: e.remote_dma_fused(tr, local_sem=T.sem[loc]), rd, [], kind="r", sem=loc, val=sum(len(x) for x in es.values()))

    def arrives(sem, wr):
        add(P, "X", None, [], wr, kind="x", sem=sem, val=NIN)

    def select(out, n, pat, op, base, wr):
        add(P, "G", lambda e: e.affine_select(out, T.ones[0:out.shape[0], 0:n], pat, op, 0.0, base, 1), [full("ones")], [wr])

    mine = slice(32 * rank, 32 * rank + 32)
    gs = group()
    dma(T.pm32[:], T.pm[:], [], [full("pm32")])
    dma(T.sP[:], T.pm[:], [], [("sP", 0, 4)])
    for i in range(2):
        dma(T.st32[:, i, :], T.st[i:8:2, :], [], [("st32", 128 * i, 128 * i + 128)], gs, 2)
    dma(T.en32[:], T.en[:], [], [full("en32")])
    dma(T.rP[rank], T.pm[mine, :], [], [("rP", rank, rank + 1)])
    vec(lambda e: e.memset(T.ones[:], 1.0), [], [full("ones")])
    act(T.Lb[:, V - 128:V], T.ones[:], [full("ones")], [("Lb", V - 128, V)], AF.Exp)
    zero("V", "Wb", 0, 1024)
    zero("V", "Lb", 0, 3072)
    zero("S", "Lb", 3072, V - 128)
    for a in range(0, 128, 32):
        select(T.tri[a:a + 32, :], 32, [[-1, 32]], A.is_ge, 0, ("tri", 0, 32, a))
    act(T.low[:], T.tri[:], [full("tri")], [full("low")], AF.Identity, scale=-1.0, bias=1.0)
    for nm, pat in (("sel8", [[-16, 8]]), ("sel32", [[-64, 2], [0, 4], [-16, 4]]), ("idn", [[-1, 128]])):
        select(T[nm][:], SCRATCH[nm][1][1], pat, A.is_equal, 0 if nm == "idn" else -OFF, full(nm))
    send(lambda k: (T.sP[k], T.rP[rank], ("sP", 0, 4)), "arrP", "locP")

    vec(lambda e: e.tensor_copy(T.pmF[:], T.pm32[:]), [full("pm32")], [full("pmF")])
    for c in range(8):
        vec(lambda e, c=c: e.transpose(T.Tm[:, c, :], T.pmF[:, c:256:8]), [full("pmF")], [("Tm", 32 * c, 32 * c + 32)])
    for i in range(2):
        act(T.C1[:, i, 32:160], T.Tm[:, :, 16 * i:16 * i + 16], [full("Tm")], [("C1", 160 * i + 32, 160 * i + 160)], AF.Exp, scale=1.0 / 64, bias=-64.0)
    vec(lambda e: e.tensor_copy(T.FL[:, :, 32:160], T.st32[:]), [full("st32")], [("FL", 0, 320, "d")])
    for i in range(2):
        act(T.O1[:, i, 32:160], T.FL[:, i, 32:160], [("FL", 0, 320, "d")], [("O1", 160 * i, 160 * i + 160), ("has", i, i + 1)], accum_out=T.has[:, i:i + 1])
    for i in range(2):
        act(T.EF[:, 32 * i:32 * i + 32], T.low[:], [full("low"), ("has", i, i + 1)], [("EF", 32 * i, 32 * i + 32)], AF.Identity, scale=T.has[:, i:i + 1])
    for i in range(2):
        vec(lambda e, i=i: e.tensor_tensor_scan(T.S1[:, 128 * i:128 * i + 128], T.FL[:, i, 32:160], T.C1[:, i, 32:160], 1.0, A.max, A.min),
            [("FL", 0, 320, "d"), ("C1", 160 * i + 32, 160 * i + 160)], [("S1", 128 * i, 128 * i + 128)])
    for i in range(2):
        c = 128 * i + 127
        vec(lambda e, i=i, c=c: e.tensor_scalar(T.E1[:, 32 * i:32 * i + 32], T.tri[:], T.S1[:, c:c + 1], None, A.max),
            [full("tri"), ("S1", c, c + 1)], [("E1", 32 * i, 32 * i + 32)])
    for i in range(2):
        vec(lambda e, i=i: e.transpose(T.C1[:, i, 0:32], T.E1[:, 32 * i:32 * i + 32]), [("E1", 32 * i, 32 * i + 32)], [("C1", 160 * i, 160 * i + 32)])
    for i in range(2):
        vec(lambda e, i=i: e.transpose(T.FL[:, i, 0:32], T.EF[:, 32 * i:32 * i + 32]), [("EF", 32 * i, 32 * i + 32)], [("FL", 0, 320, "t%d" % i)])
    for i in range(2):
        vec(lambda e, i=i: e.tensor_tensor_scan(T.O1[:, i, :], T.FL[:, i, :], T.C1[:, i, :], 1.0, A.max, A.min),
            [full("FL"), ("C1", 160 * i, 160 * i + 160)], [("O1", 160 * i, 160 * i + 160)])
    gs, go, gr = group(), group(), group()
    for i in range(2):
        dma(T.sF[:, 64 * i:64 * i + 64, :], T.FL[:, i, 32:160], [("FL", 0, 320, "d")], [("sF", 0, 4, i)], gs, 2)
        dma(T.rF[rank, 64 * i:64 * i + 64, :], T.FL[mine, i, 32:160], [("FL", 0, 320, "d")], [("rF", rank, rank + 1, i)], go, 2)
    for i in range(2):
        dma(T.Lb[16 * i + OFF:128:32, :], T.O1[:, i, 32:160], [("O1", 160 * i, 160 * i + 160)], [("Lb", 0, V, i)], gr, 2)
    send(lambda k: (T.sF[k], T.rF[rank], ("sF", 0, 4)), "arrS", "locS")
    vec(lambda e: e.tensor_copy(T.LA[:], T.en32[:]), [full("en32")], [full("LA")])
    dma(T.sE[:], T.LA[:], [full("LA")], [("sE", 0, 4)])
    dma(T.rE[rank], T.LA[mine, :], [full("LA")], [("rE", rank, rank + 1)])
    nA = PARTS["A"][2]
    act(T.Wb[:, 1024:1152], T.ones[:], [full("ones")], [("Wb", 1024, 1152)], AF.Ln)
    zero("V", "Wb", 1152, 128 * max(nA, CUT1[1]))
    zero("V", "mf", 0, 256)
    vec(lambda e: e.memset(T.mf[:, 0:256:4], 1.0), [], [full("mf")])

    def fetch(sem, src, dst, cols, rows=False):
        arrives(sem, [(src, k, k + 1) for k in others])
        gl, h = group(), SCRATCH[src][1][1] // 2
        for grp in range(2):
            out = T[dst][64 * grp + OFF:64 * grp + 64:16, :] if rows else T[dst][64 * grp:64 * grp + 64, cols[0]:cols[1]]
            dma(out, T[src][:, h * grp:h * grp + h, :], [(src, 0, 4)], [(dst,) + cols + (grp,)], gl, 2)

    fetch("arrP", "rP", "PB", (0, 256))
    H = CUT1[1]

    def out1(j, q):
        bank, name, w = "psT%d" % j, "sb%d" % j, 2 * (CUT1[j + 1] - CUT1[j])
        copy(q, T[name][:, 0:4 * w], T[bank][:, 0:4 * w], [(bank, 0, 512)], [(name, 0, 4 * w)])
        own = (name, (4 + rank) * w, (5 + rank) * w)
        send(lambda k: (T[name][:, w * k:w * k + w], T[name][:, own[1]:own[2]], (name, w * k, w * k + w)), "arrX%d" % j, "locX%d" % j)

    def in1(j):
        name, w = "sb%d" % j, 2 * (CUT1[j + 1] - CUT1[j])
        arrives("arrX%d" % j, [(name, (4 + k) * w, (5 + k) * w) for k in others])
        vec(lambda e: e.tensor_tensor(T.A1[:, 0:2 * w], T[name][:, 4 * w:6 * w], T[name][:, 6 * w:8 * w], A.min), [(name, 4 * w, 8 * w)], [full("A1")])
        return w

    def turn1(v):
        j = max(i for i, c in enumerate(CUT1) if c <= v)
        bank, n, rd = "psT%d" % j, CUT1[j + 1] - CUT1[j], [("stB", 128 * v, 128 * v + 128), full("sel8")]
        if j == 0:
            pe(lambda e: e.matmul(T[bank][:, v:8 * n:n], T.stB[:, 128 * v:128 * v + 128], T.sel8[:], True, True), rd, [(bank, 0, 512, v)])
        else:
            for i in range(2):
                c = 2 * (v - CUT1[j]) + i
                pe(lambda e, c=c, i=i: e.matmul(T[bank][:, c:8 * n:2 * n], T.stB[:, 128 * v:128 * v + 128], T.sel8[:, i:8:2], True, True), rd, [(bank, 0, 512, c)])

    for x in BACK1:
        if x[0] == "out":
            out1(x[1], x[2])
        else:
            gather(x[0], "stB", 128 * x[1], 128 * x[2], "Lb", 0, "LA")
            for v in range(x[1], x[2]):
                turn1(v)
    send(lambda k: (T.sE[k], T.rE[rank], ("sE", 0, 4)), "arrL", "locL")
    for j in range(len(CUT1) - 1):
        name, w = "sb%d" % j, 2 * (CUT1[j + 1] - CUT1[j])
        copy("S", T[name][:, (4 + rank) * w:(5 + rank) * w], T[name][:, w * rank:w * rank + w], [(name, w * rank, w * rank + w)], [(name, (4 + rank) * w, (5 + rank) * w)])
    vec(lambda e: e.tensor_copy(T.LB[:, 0:256], T.PB[:]), [full("PB")], [("LB", 0, 256)])
    fetch("arrS", "rF", "stB", (0, V), True)
    add(P, "G", lambda e: e.iota(T.refv[:], [[128, 32], [0, 2]], int(MAGIC), 1, allow_small_or_imprecise_dtypes=True), [], [full("refv")])
    zero("G", "WF", 0, 8208)
    in1(0)
    vec(lambda e: e.tensor_tensor(T.M1[:, 0:2 * H], T.A1[:, 0:2 * H], T.A1[:, 2 * H:4 * H], A.min), [full("A1")], [full("M1")])
    pe(lambda e: e.transpose(T.psR[0:2 * H, 0:128], T.M1[:, 0:2 * H], T.idn[:]), [full("M1"), full("idn")], [("psR", 0, 128)])
    copy("V", T.R4[0:2 * H, :], T.psR[0:2 * H, 0:128], [("psR", 0, 128)], [full("R4")])
    gr = group()
    for k in range(N):
        dma(T.Wb[16 * k + OFF:128:64, 0:128 * H], T.R4[0:2 * H, :], [full("R4")], [("Wb", 0, 128 * H, k)], gr, 4)
    fetch("arrL", "rE", "LB", (256, 512))
    dma(T.sC[:], T.refv[:, 0:2], [full("refv")], [("sC", 0, 1)])
    for j in range(1, len(CUT1) - 1):
        w, a, b = in1(j), 128 * CUT1[j], 128 * CUT1[j + 1]
        for k in range(N):
            vec(lambda e, k=k, w=w, a=a, b=b: e.tensor_tensor(T.Lb[:, a + 16 * k + OFF:b:64], T.A1[:, 0:w], T.A1[:, w:2 * w], A.min), [full("A1")], [("Lb", a, b, k)])
        mine1 = [(i, x) for i, x in enumerate(SPREAD1) if a <= 128 * x[1] < b]
        for i, (q, lo, hi) in mine1:
            spread("psE%d" % i, lo, hi)
        for i, (q, lo, hi) in mine1:
            window_copy(q, "psE%d" % i, lo, hi)

    chunks, free = {}, ["psE0", "psE1", "psE2", "psE3", "psR"]
    for x in "BCDE":
        a, m, b = PARTS[x]
        c = a + WSHARE[x]
        chunks[x] = [(q, lo, hi, free.pop(0)) for q, lo, hi in (("S", a, c), ("V", c, b)) if hi > lo]

    def part(x, w, q):
        a, m, b = PARTS[x]
        if w == "g":
            back(q, *((a, m) if q == "V" else (m, b)))
        elif w == "t":
            turn(TURN[x], a, b, "sel32", 32)
        elif w == "f":
            min4(TURN[x], 32 * (b - a), T.Lb[:, 128 * a:128 * b:4], ("Lb", 128 * a, 128 * b))
        else:
            for q2, lo, hi, bank in chunks[x]:
                if w == "e":
                    spread(bank, lo, hi)
                elif q2 == q:
                    window_copy(q, bank, lo, hi)

    def first_part(w, q):
        b = nA
        if w == "g":
            lo, hi = FIRST[q]
            back(q[0], lo, hi)
            for v in range(lo, hi):
                for grp in range(2):
                    c = 4 * (b * grp + v)
                    pe(lambda e, v=v, c=c, h=4 * grp: e.matmul(T.psT0[:, c:c + 4], T.u[:, 128 * v:128 * v + 128], T.sel8[:, h:h + 4], True, True),
                       [("u", 128 * v, 128 * v + 128), full("sel8")], [("psT0", c, c + 4)])
        elif w == "f":
            min4("psT0", 8 * b, T.l1[:, 0:8 * b], ("l1", 0, 8 * b))
        elif w == "r":
            pe(lambda e: e.transpose(T.psR[0:2 * b, 0:128], T.l1[:, 3:8 * b:4], T.idn[:]), [("l1", 0, 8 * b), full("idn")], [("psR", 0, 128)])
        else:
            copy(q, T.R4[0:2 * b, :], T.psR[0:2 * b, 0:128], [("psR", 0, 128)], [full("R4")])
            gr = group()
            for k in range(N):
                dma(T.Wb[16 * k + OFF:128:64, 0:128 * b], T.R4[0:2 * b, :], [full("R4")], [("Wb", 0, 128 * b, k)], gr, 4)

    for r in range(2, R):
        class_minima()
        for x in ORDER.split():
            if x[0] == "A":
                first_part(x[1], x[2:])
            else:
                part(x[0], x[1], x[2:])
    class_minima()

    def fold(bank, a, m, b):
        min4(bank, 8 * (b - a), T.l1[:, 8 * a:8 * b], ("l1", 8 * a, 8 * b))

    def logs(h):
        a, b = WF * h, WF * h + WF
        act(T.dL[:, a:b], T.l1[:, 4 * a + 3:4 * b:4], [("l1", 4 * a, 4 * b)], [("dL", a, b)], AF.Ln, scale=math.exp(32.0))

    def numbers(h):
        part = ("vF", WF * h, WF * h + WF)
        vec(lambda e: e.tensor_scalar(T.vF[:, part[1]:part[2]], T.dL[:, part[1]:part[2]], 64.0, MAGIC + 2048.0, A.mult, A.add), [("dL", part[1], part[2])], [part])
        send(lambda k: (T.vF[:, part[1]:part[2]], T.rland[h, rank], part), "arrF%d" % h, "locF%d" % h)
        dma(T.rland[h, rank], T.vF[:, part[1]:part[2]], [part], [("rland", 4 * h + rank, 4 * h + rank + 1)])

    for x in ORDER6.split():
        i = int(x[1])
        bank, a, m, b = LAST[i]
        if x[0] == "V":
            back("V", a, m)
        elif x[0] == "S":
            back("S", m, b)
        elif x[0] == "t":
            turn(bank, a, b, "sel8", 8)
        elif x[0] == "f":
            fold(bank, a, m, b)
        elif x[0] == "l":
            logs(i)
        else:
            numbers(i)
    vec(lambda e: e.tensor_tensor(T.eq[:], T.vF[:], T.refv[:], A.is_equal), [full("vF"), full("refv")], [full("eq")])
    pe(lambda e: e.matmul(T.psT1[0:1, 0:64], T.ones[:, 0:1], T.eq[:], True, True), [full("eq"), full("ones")], [("psT1", 0, 64)])
    for i in range(2):
        act(T.dL[0:1, 0:32], T.psT1[0:1, i:64:2], [("psT1", 0, 64)], [("dL", 0, 32), ("cn", i, i + 1)], accum_out=T.cn[0:1, i:i + 1])
    dma(T.sC[0:1, :], T.cn[0:1, 0:2], [("cn", 0, 2)], [("sC", 0, 1)])
    dma(T.rC[rank, 0:1, :], T.cn[0:1, 0:2], [("cn", 0, 2)], [("rC", rank, rank + 1)])
    send(lambda k: (T.sC[:], T.rC[rank], ("sC", 0, 1)), "arrC", "locC")
    vec(lambda e: e.tensor_scalar(T.i1[:], T.pm32[:], 7, None, A.arith_shift_right), [full("pm32")], [full("i1")])
    vec(lambda e: e.tensor_scalar(T.i2[:], T.pm32[:], WF, 1, A.mult, A.add), [full("pm32")], [full("i2")])
    if NF == 2:
        vec(lambda e: e.tensor_scalar(T.i3[:], T.pm32[:], 2048, 4072, A.is_ge, A.mult), [full("pm32")], [full("i3")])
    vec(lambda e: e.tensor_scalar(T.i1[:], T.i1[:], 2 - 128 * WF, None, A.mult), [full("i1")], [full("i1")])
    for a in ("i1", "i3")[:NF]:
        vec(lambda e, a=a: e.tensor_tensor(T.i2[:], T[a][:], T.i2[:], A.add), [full(a), full("i2")], [full("i2")])
    vec(lambda e: e.tensor_copy(T.LW[:], T.i2[:]), [full("i2")], [full("LW")])

    for h in range(NF):
        arrives("arrF%d" % h, [("rland", 4 * h + k, 4 * h + k + 1) for k in others])
        gf, c = group(), 4104 * h + 1
        for i in range(2):
            dma(T.WF[16 * i:128:32, c - i:c + 128 * WF - i], T.rland[h], [("rland", 4 * h, 4 * h + 4)], [("WF", c - 1, c + 128 * WF, i)], gf, 2)

    def final(q, a, b):
        out, win = T.Yb[:, a:b], T.WF[:, 0:8208].indirect(T.LW[:, a // 16:b // 16])
        rd, wr = [full("WF"), ("LW", a // 16, b // 16)], [("Yb", a, b)]
        if q == "V":
            vec(lambda e: e.tensor_scalar(out, win, -MAGIC, None, A.add), rd, wr)
        else:
            act(out, win, rd, wr, AF.Identity, bias=-MAGIC)

    for a, b in ((0, 1024), (1024, 2048)):
        for q, h in (("V", 0), ("S", 2048)):
            final(q, h + a, h + b)
            dma(T.y[:, h + a:h + b], T.Yb[0:128:16, h + a:h + b], [("Yb", h + a, h + b)], [])
    arrives("arrC", [("rC", k, k + 1) for k in others])
    dma(T.cnt[:], T.rC[:, 0, :], [("rC", 0, 4)], [], q="S")

    emit(P, g, T)
